import numpy as np, ml_dtypes
CORES = [16,18,20,22]
N = 4
BF = ml_dtypes.bfloat16
V, TY, LN, SL, RT, RO, ST = 2048, 1024, 512, 64, 32, 4, 640
WT = 1 + 10 * np.arange(16)
def cand(u):
    return ((u * u >> 5) + u + np.arange(16)[:, None] * (2 * u + 1)) & (V - 1)
def pack(w, x, q, s, h, v, t):
    i = lambda a, n: np.ascontiguousarray(a).reshape(N, -1, n).astype(np.int32)
    b = lambda a, n: np.ascontiguousarray(a).reshape(N, -1, n).astype(np.float32).astype(BF)
    return {"wd": i(w, V), "xs": b(x, V), "rq": i(q, TY), "sg": b(s, TY), "hy": i(h, V), "vf": i(v, V), "th": i(t, 1)}
def world(rng, A, top, size, twin, noise, pw, wrong, harm):
    w = np.zeros((N, 8, 16, V), np.int64); x = w.copy(); q = np.zeros((N, 8, 16, TY), np.int64); s = q.copy(); h = np.zeros((N, 8, V), np.int64); tt = h.copy()
    for r in range(N):
        for g in range(8):
            live = rng.permutation(TY)[:A]
            sa = rng.integers(0, top + 1, (16, TY)) >> rng.integers(0, size + 1, (1, TY))
            sa[:, live[1::2]] = np.clip(sa[:, live[0::2]] + rng.integers(-twin, twin + 1, (16, A // 2)), 0, 255)
            qa = np.where(rng.random((16, TY)) < rng.random((1, TY)), live[(A * rng.random((16, TY)) ** pw).astype(np.int64)], TY)
            k = rng.permutation(np.concatenate([np.arange(A), (A * rng.random(V - A) ** pw).astype(np.int64)]))
            o = np.argsort(k, kind="stable"); n = np.bincount(k, minlength=A); b = np.add.accumulate(n) - n
            back = np.zeros(TY + 1, np.int64); back[live] = np.arange(A)
            need = qa[:, live[k]]; kk = back[need]
            wa = o[b[kk] + (n[kk] * rng.random((16, V)) ** pw).astype(np.int64)]
            p = rng.choice(np.array([0.0, 0.0, 0.0, 0.0, 0.0, 0.0, 0.15, 0.15, 0.15, 0.5]), V) * harm
            wa = np.where((need == TY) | (rng.random((16, V)) < p), rng.integers(0, V, (16, V)), wa)
            off = np.where(rng.random(V) < 0.5, live[rng.integers(0, A, V)], rng.integers(0, TY, V))
            h[r, g] = np.where(rng.random(V) < wrong[r, g], off, live[k]); tt[r, g] = live[k]
            x[r, g] = np.clip(sa[:, live[k]] + rng.integers(-noise, noise + 1, (16, V)), 0, 255)
            w[r, g], q[r, g], s[r, g] = wa, qa, sa
    return w, x, q, s, h, tt
def setup_inputs(rng):
    wrong = rng.choice(np.array([0.004, 0.02, 0.06, 0.15]), (N, 8))
    w, x, q, s, h, tt = world(rng, min(V, TY) // 2, 255, 0, 3, 4, 1, wrong, 1.0)
    v = rng.random((N, 8, V)) < rng.choice(np.array([0.02, 0.2, 0.5, 0.85]), (N, 8, 1))
    t = 40 + (1200 * rng.random((N, 8, 16)) ** 2).astype(np.int64)
    return pack(w, x, q, s, h, v, t)
def setup_inputs_spread(rng):
    w, x, q, s, h, tt = world(rng, min(V, TY) // 2, 255, 7, 2, 4, 3, 0.2 * rng.random((N, 8)), 1.0)
    v = rng.random((N, 8, V)) < rng.random((N, 8, 1))
    t = np.minimum(np.exp2(12 * rng.random((N, 8, 16))).astype(np.int64) - 1, 4080)
    return pack(w, x, q, s, h, v, t)
def setup_inputs_ties(rng):
    w, x, q, s, h, tt = world(rng, 8, 150, 0, 0, 0, 1, rng.choice(np.array([0.1, 0.3, 0.5]), (N, 8)), 0.5)
    near = np.array([49, 50, 51])
    x = np.take_along_axis(s, np.broadcast_to(tt[:, :, None, :], (N, 8, 16, V)), 3)
    x = x + (np.arange(16)[:, None] == rng.integers(0, 16, (N, 8, 1, V))) * rng.choice(near, (N, 8, 1, V))
    v = rng.random((N, 8, V)) < rng.choice(np.array([0.1, 0.4, 0.6]), (N, 8, 1))
    return pack(w, x, q, s, h, v, rng.choice(near, (N, 8, 16)))
def setup_inputs_ends(rng):
    def two(lo, hi, *sh): return np.where(rng.random(sh) < 0.5, lo, hi)
    x = np.where(rng.random((N, 8, 1, V)) < 0.5, two(0, 255, N, 8, 1, V), two(0, 255, N, 8, 16, V))
    s = np.where(rng.random((N, 8, 1, TY)) < 0.5, two(0, 255, N, 8, 1, TY), two(0, 255, N, 8, 16, TY))
    h = np.where(rng.random((N, 8, V)) < 0.9, two(0, TY - 1, N, 8, V), rng.integers(0, TY, (N, 8, V)))
    v = (rng.random((N, 8, V)) < 0.4).astype(np.int64)
    w = np.where(rng.random((N, 8, 16, V)) < 0.8, two(0, V - 1, N, 8, 16, V), rng.integers(0, V, (N, 8, 16, V)))
    q = np.where(rng.random((N, 8, 16, TY)) < 0.7, two(0, TY, N, 8, 16, TY), TY - 1)
    for c in (0, TY - 1): q[..., c] = np.where(rng.random((N, 8, 16)) < 0.85, two(0, TY - 1, N, 8, 16), TY)
    z = np.stack([rng.permutation(np.array([2, 3, 4, 5, 6, 8, 12, 16])) for r in range(N)]); z[:, 7] = 5
    t = np.where(np.argsort(rng.random((N, 8, 16)), axis=-1) < z[..., None], 0, 4080)
    c = cand(np.array([(255 * 1216) & (V - 1)]))[:, 0]
    v[:, 7, 0] = 1; v[:, 7, V - 1] = 0; v[:, 7, c[:2]] = 0; v[:, 7, c[2]] = 1; v[:, 7, c[15]] = 1
    x[:, 7] = np.where(v[:, 7] == 1, 0, 255)[:, None, :]
    lo = two(0, 255, N, 8, 1); lo[:, 7] = 0
    x[..., 0] = lo; x[..., V - 1] = 255 - lo; s[..., 0] = 255 - lo
    s[..., TY - 1] = np.where(rng.random((N, 8, 1)) < 0.5, lo, 255 - lo); s[:, 7, :, TY - 1] = 0
    h[..., 0] = TY - 1; h[..., V - 1] = 0
    q[0, :, 0] = TY; t[0] = 4080; t[0, :, 0] = 0
    return pack(w, x, q, s, h, v, t)
def setup_inputs_corners(rng):
    w0 = np.zeros((N, 8, 16, V), np.int64); x0 = w0.copy(); q0 = np.zeros((N, 8, 16, TY), np.int64); s0 = q0.copy(); h0 = np.zeros((N, 8, V), np.int64); v0 = h0.copy()
    all_ = V - 16
    plan_u = (all_, LN, LN + 1, LN - 1, 1, 0, all_, all_); plan_p = (SL, SL + 1, SL - 1, LN, 1, 0, 0, SL); plan_t = (RT, RT + 1, RT - 1, 0, 0, 0, LN, RT)
    for r in range(N):
        for g in range(8):
            live = rng.permutation(TY)[:32]; s = rng.integers(0, 256, (16, TY)); s[:, live[1::2]] = s[:, live[0::2]]
            q = np.where(rng.random((16, TY)) < 0.6, live[rng.integers(0, 32, (16, TY))], TY)
            q[np.array([0, 3, 7, 11])] = live[rng.integers(0, 32, (4, TY))]; q[15, live] = live
            z = 1 + rng.permutation(V - 2)[:16]; reg = np.setdiff1d(np.arange(V), z)
            k = rng.permutation(np.concatenate([np.arange(32), rng.integers(0, 32, V - 48)]))
            o = np.argsort(k, kind="stable"); n = np.bincount(k, minlength=32); b = np.add.accumulate(n) - n
            back = np.zeros(TY + 1, np.int64); back[live] = np.arange(32)
            pairs = np.arange(16)
            h = np.zeros(V, np.int64); h[reg] = live[k]; h[z] = live[(2 * pairs + 2) % 32]
            x = np.zeros((16, V), np.int64); x[:, reg] = np.clip(s[:, live[k]] + rng.integers(-3, 4, (16, V - 16)), 0, 255); x[:, z] = s[:, live[2 * pairs]]
            w = rng.integers(0, V, (16, V)); need = q[:, h[reg]]; kk = back[need]
            wr = np.where(need == TY, w[:, reg], reg[o[b[kk] + (n[kk] * rng.random(kk.shape)).astype(np.int64)]])
            wr[15] = np.where(rng.random(V - 16) < 0.5, reg, wr[15])
            for e in (0, V - 17): wr = np.where((need < TY) & (kk == k[e]) & (rng.random(kk.shape) < 0.3), reg[e], wr)
            w[:, reg] = wr
            if r == 0: nu, n1, n2 = plan_u[g], plan_p[g], plan_t[g]
            else:
                nu = int(rng.choice(np.array([0, 1, LN - 1, LN, LN, LN + 1, all_, all_])))
                n1 = int(rng.choice(np.array([0, 1, SL - 1, SL, SL + 1, LN - RT - 1]))); n2 = int(rng.choice(np.array([0, 1, RT - 1, RT, RT + 1, LN])))
            on = np.sort(rng.permutation(reg)[:nu]); v = np.ones(V, np.int64); v[on] = 0
            la = rng.permutation(on[:LN]); m = len(la); n1 = min(n1, m); n2 = min(n2, m - n1); n3 = min(m - n1 - n2, int(rng.integers(0, 40)))
            nd = np.zeros(m, np.int64); nd[:n1] = rng.integers(1, 4, n1); nd[n1 + n2:n1 + n2 + n3] = rng.integers(4, 6, n3)
            need = q[:, h[la]]; kk = back[need]
            at = np.argsort(np.argsort(np.where(need < TY, rng.random(need.shape), 2.0), axis=0), axis=0)
            kb = 2 * ((kk // 2 + 1 + rng.integers(0, 15, kk.shape)) % 16) + rng.integers(0, 2, kk.shape)
            new = np.where(at < nd, reg[o[b[kb] + (n[kb] * rng.random(kb.shape)).astype(np.int64)]], w[:, la])
            re_ = (np.arange(m) >= n1) & (np.arange(m) < n1 + n2)
            w[:, la] = np.where((at == 0) & re_, z[kk // 2], new)
            w0[r, g], x0[r, g], q0[r, g], s0[r, g], h0[r, g], v0[r, g] = w, x, q, s, h, v
    return pack(w0, x0, q0, s0, h0, v0, rng.choice(np.array([0, 1, 30, 60]), (N, 8, 16)))
def setup_inputs_full(rng):
    w = rng.integers(0, V, (N, 8, 16, V)); x = np.zeros((N, 8, 16, V), np.int64); q = np.full((N, 8, 16, TY), TY); s = rng.integers(0, 256, (N, 8, 16, TY))
    h = np.zeros((N, 8, V), np.int64); v = h.copy(); M = TY - 24; i = np.arange(V); edge = max(ST, LN) + LN; first = int(rng.integers(0, N))
    for a in range(N):
        r = (first + a) % N; role = a % 4; lo, hi = ((200, 241), (10, 41), (40, 121), (40, 121))[role]
        for g in range(8):
            ty = rng.permutation(TY); rest = ty[24:]
            b = rng.integers(lo, hi, (16, 1)); x[r, g] = b + rng.integers(-2, 3, (16, V))
            far = rng.integers(0, 21, (16, 8)); s[r, g][:, ty[:8]] = far if role == 0 else 255 - far
            s[r, g][:, ty[8:16]] = b + (2 * rng.integers(0, 2, (16, 8)) - 1) * rng.integers(5, 8, (16, 8)); s[r, g][:, ty[16:24]] = b
            sort = np.arange(M) % 4; at = np.argsort(rng.random((16, M)), axis=0)
            cnt = np.where(sort == 1, rng.integers(1, 4, M), np.where(sort == 2, rng.integers(1, 9, M), np.where(sort == 3, 1, 0)))
            pick = np.where(sort == 3, np.arange(M) // 4 % 8, rng.integers(0, 8, (16, M)))
            q[r, g][:, rest] = np.where(at < cnt, ty[8 * np.maximum(sort - 1, 0) + pick], TY)
            c = rng.integers(0, 4, V)
            if role == 0:
                c[:LN] = 1; v[r, g, LN:] = rng.random(V - LN) < 0.5
                if g % 4 == 3: c[:256] = 0
            elif role == 1: v[r, g] = rng.random(V) < 0.85
            elif role == 2: c = np.where(i < LN, 0, 2)
            else: c = np.where(i < edge, 1, 2); c[rng.permutation(LN)[:int(rng.integers(20, 29))]] = 0
            y = 4 * rng.integers(0, M // 4, V) + c
            if role == 2:
                o = np.arange(256, LN - 1, 4); goal = LN + rng.permutation(V - LN)[:len(o)]
                for k in (0, 1):
                    y[o + k] = 4 * (2 * rng.integers(0, M // 8, len(o)) + k) + 3
                    w[r, g, np.argmin(at[:, y[o + k]], axis=0), o + k] = goal
            h[r, g] = rest[y]
    for a in range(0, N - 1, 4):
        r, e = (first + a) % N, (first + a + 1) % N
        for g in (3, 7):
            k = np.arange(255 + SL, 255, -1); c = cand(np.add.reduce(WT[:, None] * x[r, g][:, k], axis=0) & (V - 1))
            top = np.max(x[e, g], axis=1) + 1; used = np.zeros(V, bool)
            for b in range(SL):
                if np.any(used[c[:, b]]): continue
                used[c[:, b]] = True; v[e, g, c[0, b]] = 1; v[e, g, c[15, b]] = 1
                x[e, g][:, c[0, b]] = top - (np.arange(16) == rng.integers(0, 16)); x[e, g][:, c[15, b]] = top
    return pack(w, x, q, s, h, v, 32 + rng.integers(0, 9, (N, 8, 16)))
def check_inputs(d):
    bad = []
    for k, lo, hi in (("wd", 0, V - 1), ("xs", 0, 255), ("rq", 0, TY), ("sg", 0, 255), ("hy", 0, TY - 1), ("vf", 0, 1), ("th", 0, 4080)):
        a = np.asarray(d[k]).astype(np.float64)
        if not (np.min(a) >= lo and np.max(a) <= hi): bad.append("range of " + k)
        elif np.any(a != np.floor(a)): bad.append("whole numbers of " + k)
    return bad
def reference(wd, xs, rq, sg, hy, vf, th):
    m = wd.astype(np.int64).reshape(N, 8, 16, V); x = xs.astype(np.float32).astype(np.int64).reshape(N, 8, 16, V)
    q = rq.astype(np.int64).reshape(N, 8, 16, TY); s = sg.astype(np.float32).astype(np.int64).reshape(N, 8, 16, TY)
    h = hy.astype(np.int64).reshape(N, 8, V); v = vf.reshape(N, 8, V) == 1; lim = th.astype(np.int64).reshape(N, 8, 16, 1)
    last = np.zeros(N, np.int64)
    for t in range(RO):
        d = 1 + t % (N - 1); order = (ST * t + np.arange(V)) % V
        m1, h1, v1 = m.copy(), h.copy(), v.copy(); now = np.zeros(N, np.int64)
        for r in range(N):
            e = (r + d) % N
            for g in range(8):
                a = order[~v[r, g][order]][:LN]
                w = m[r, g][:, a]; need = q[r, g][:, h[r, g][a]]
                other = (need < TY) & (h[r, g][w] != need)
                far = np.add.reduce(np.abs(x[r, g][:, w] - s[r, g][:, np.minimum(need, TY - 1)]), axis=0)
                fail = other & (far > lim[r, g] + (last[r] & 255))
                n = np.add.reduce(fail.astype(np.int64), axis=0); good = n == 0; much = n > 3
                now[r] += np.count_nonzero(good)
                v1[r, g, a[good]] = True
                y = h[r, g][a[much]]; h1[r, g, a[much]] = ((y * y >> 4) + 5 * y + n[much]) & (TY - 1)
                i = np.flatnonzero((n > 0) & (n < 4))[:SL]
                if len(i) > 0:
                    z = x[r, g][:, a[i]]; u = np.add.reduce(WT[:, None] * z, axis=0) & (V - 1); c = cand(u); k = np.arange(len(i))
                    gap = np.add.reduce(np.abs(x[e, g][:, c] - z[:, None, :]), axis=0)
                    gap = np.where(v[e, g][c], gap, 4096); b = np.argmin(gap, axis=0)
                    take = fail[:, i] & (gap[b, k] < 4096)
                    m1[r, g][:, a[i]] = np.where(take, m[e, g][:, c[b, k]], w[:, i])
                j = np.flatnonzero(good & np.any(other, axis=0))[:RT]
                if len(j) > 0:
                    p = np.argmax(other[:, j], axis=0); name, one = np.unique(w[p, j], return_index=True)
                    h1[r, g, name] = need[p, j][one]; v1[r, g, name] = False
        m, h, v, last = m1, h1, v1, now
    return {"ym": m.reshape(N, 128, V).astype(np.float32), "yh": h.astype(np.float32), "yv": v.astype(np.float32)}

@@ -1,0 +1,655 @@
+from concourse.mybir import AluOpType as OP, AxisListType, ActivationFunctionType as AF
+
+V, TY, LN, SL, RT, RO, ST0 = 2048, 1024, 512, 64, 32, 4, 640
+NB = 160
+FBW = 8704
+STW = 2736
+DUMP = 2688
+MARK = 2736
+WDW = 2752
+XSW = 2640
+NCH = 4
+CW = LN // NCH
+TF = (1, 2)
+SB = 2
+
+BFB, F32, I32, U16 = "bfloat16", "float32", "int32", "uint16"
+SCRATCH = {}
+
+
+def _buf(name, cols, d, where="sbuf"):
+    SCRATCH[name] = (where, [128, cols], d)
+
+
+for _n, _c, _d in [
+    ("WI", V, I32), ("WD", WDW, F32), ("XS", XSW, BFB), ("RQ", 1040, I32), ("SG", 1040, BFB),
+    ("HS", 128, I32), ("VS", 128, I32), ("TH", 1, I32), ("HX", 256, I32),
+    ("HB3", 384, BFB), ("ST", STW, BFB), ("SVB", V, BFB), ("FB", FBW, BFB),
+    ("GM", 8, BFB), ("GG", 128, BFB), ("ID", 128, BFB), ("ON", 128, BFB), ("ZZ", 144 * 9, BFB), ("WV", 2048, BFB), ("PWM", 2048, BFB),
+    ("MX", 128 * 17, BFB), ("GF", 128, F32), ("RF", 128, F32), ("SF", 128, F32),
+    ("PI", 1, I32), ("PA", 1, I32), ("PC", 1, F32), ("PC1", 1, F32), ("CO", 32, F32), ("RI", 16, F32), ("CMI", 128, BFB), ("CMJ", 128, BFB), ("GK", 128, BFB),
+    ("JR", 512, F32), ("BR", NB, BFB), ("ER", NB, BFB), ("ZR", NB, F32), ("DG", 64, F32), ("TR", 64, F32), ("RB", 4, F32), ("RC", 4, F32), ("RE", 2, F32),
+    ("M16", 16, F32), ("M64", 64, F32), ("YI", 64 * 7, I32), ("YD", 128, BFB), ("GTB", 1040, BFB), ("YHM", 8, BFB),
+    ("PIN", NB, BFB), ("BPI", NB, F32), ("BPX", NB, F32), ("PW", NB, F32), ("EM", NB, BFB), ("EMC", NB, BFB), ("OFF", 10, F32), ("OF16", 10, U16),
+    ("FR", 512, BFB), ("FL16", 32, U16), ("AJ", 96, BFB), ("E", 512, BFB), ("A16", 32, U16),
+    ("XR0", 576, F32), ("YG", 512, BFB), ("Y16", 32, U16), ("GB", 512, BFB),
+    ("KF", 576, F32), ("K16", 512, U16), ("DA", 512, BFB), ("WF", 576, F32), ("W16", 512, U16), ("LIM", 2, F32),
+    ("H0", 16 * CW, BFB), ("H1", 16 * CW, BFB), ("D0", 16 * CW, BFB), ("D1", 16 * CW, BFB), ("R0", 16 * CW, BFB), ("R1", 16 * CW, BFB),
+    ("O0", 576, BFB), ("FF", 576, BFB), ("PM", 512, BFB), ("PP", 512, BFB), ("MU", 512, BFB), ("T2", 512, F32), ("QQ", 512, I32), ("DD", 512, I32),
+    ("NG", 512, BFB), ("MN", 512, BFB), ("RP", 512, BFB), ("JK", 512, BFB), ("AC", 8, F32),
+    ("PL16", 2, U16), ("WKG", 160, F32), ("OKR", 96, BFB), ("FI", 32, F32),
+    ("WW", 10, F32), ("EQ", 128, F32), ("OX16", 2, U16), ("KI", 64, I32), ("GC", 3, F32), ("BI", 2, I32),
+    ("RN", 20, F32), ("RL16", 4, U16), ("XG", 128, F32), ("X4", 16, F32), ("RA16", 4, U16),
+    ("UI", 32, I32), ("BS", 8, F32), ("CI", 128, I32), ("C16", 64, U16), ("DX", 1024, BFB), ("RX2", 1024, BFB), ("VG", 1024, BFB),
+    ("KEY", 64, F32), ("KM", 16, F32), ("BB16", 4, U16), ("FLG", 64, BFB), ("WO", 320, F32), ("YO", V, F32),
+]:
+    _buf(_n, _c, _d)
+for _k in range(NCH): _buf("B%d" % _k, 16 * CW, BFB)
+for _t in range(RO):
+    _buf("XQ%d" % _t, SL, BFB)
+    _buf("QX%d" % _t, SL, BFB)
+    _buf("WR%d" % _t, SL, F32)
+    _buf("QW%d" % _t, SL, F32)
+PART = {}
+for _k, _n in enumerate(("Z", "ZM", "Z2", "Z32", "ZM16", "ZY", "ZU", "ZV", "Z0")): PART[_n] = ("ZZ", 144 * _k, 144)
+_buf("Z016", 144, BFB)
+for _k, _n in enumerate(("LT", "GR2", "G016", "G32", "GN", "RS", "RS32", "RSN", "YR", "YRN", "GR", "I8", "I8N", "US", "PL", "GR3")): PART[_n] = ("MX", 128 * _k, 128)
+for _n, _b, _w, _l in (("HXA", "HX", 128, 0), ("HXB", "HX", 128, 1), ("A1", "AJ", 32, 1), ("A2", "AJ", 32, 2), ("AJ0", "AJ", 32, 0),
+                       ("WG", "WKG", 32, 0), ("KG", "WKG", 32, 1), ("WK", "WKG", 32, 2), ("KK", "WKG", 32, 3), ("WDG", "WKG", 32, 4),
+                       ("OG", "OKR", 32, 0), ("KL", "OKR", 32, 1), ("OR", "OKR", 32, 2), ("EQ1", "EQ", 64, 0), ("EQ2", "EQ", 64, 1),
+                       ("W2", "WW", 2, 0), ("DU", "WW", 2, 1), ("DE", "WW", 2, 2), ("DE2", "WW", 2, 3), ("OX", "WW", 2, 4),
+                       ("KI1", "KI", 32, 0), ("KD", "KI", 32, 1), ("LM", "LIM", 1, 0), ("LB0", "LIM", 1, 1),
+                       ("GC1", "GC", 1, 0), ("GP", "GC", 1, 1), ("GS", "GC", 1, 2), ("BI1", "BI", 1, 0), ("BJ", "BI", 1, 1),
+                       ("RN1", "RN", 4, 0), ("RM", "RN", 4, 1), ("RK", "RN", 4, 2), ("RL", "RN", 4, 3), ("RX", "RN", 4, 4),
+                       ("XG1", "XG", 64, 0), ("XD", "XG", 64, 1), ("X1", "X4", 4, 0), ("X2", "X4", 4, 1), ("X3", "X4", 4, 2), ("X5", "X4", 4, 3),
+                       ("UI1", "UI", 4, 0), ("UA", "UI", 4, 1), ("UU", "UI", 4, 2), ("UV", "UI", 4, 3), ("MI", "UI", 4, 4), ("MJ", "UI", 4, 5), ("P2", "UI", 4, 6), ("P3", "UI", 4, 7),
+                       ("BS1", "BS", 4, 0), ("TM", "BS", 4, 1), ("CI1", "CI", 64, 0), ("CA", "CI", 64, 1),
+                       ("KM1", "KM", 4, 0), ("P1", "KM", 4, 1), ("NN", "KM", 4, 2), ("P4", "KM", 4, 3),
+                       ("WO1", "WO", 64, 0), ("MK", "WO", 64, 1), ("FM", "WO", 64, 2), ("DW", "WO", 64, 3), ("DM", "WO", 64, 4),
+                       ("YI0", "YI", 64, 0), ("YJ", "YI", 64, 1), ("Y2", "YI", 64, 2), ("Y3", "YI", 64, 3), ("Y4", "YI", 64, 4), ("Y5", "YI", 64, 5), ("Y6", "YI", 64, 6)):
+    PART[_n] = (_b, _w * _l, _w)
+
+
+def _pack(name, parts):
+    d, a = SCRATCH[parts[0]][2], 0
+    for p in parts:
+        w = SCRATCH.pop(p)[1][1]
+        PART[p] = (name, a, w)
+        a += w
+    _buf(name, a, d)
+
+
+_pack("REQ", ["XQ%d" % t for t in range(RO)] + ["QX%d" % t for t in range(RO)])
+_pack("REP", ["WR%d" % t for t in range(RO)] + ["QW%d" % t for t in range(RO)])
+_pack("CHK", ["B%d" % k for k in range(NCH)] + ["H0", "H1", "D0", "D1", "R0", "R1"])
+_pack("CF", ["JR", "ZR", "DG", "TR", "M64", "M16", "RI", "CO", "RB", "RC", "RE", "PC", "PC1"])
+_pack("CB", ["BR", "ER", "CMI", "CMJ", "GK", "GG", "ID", "ON"])
+PS = ["DA_", "DB_", "HA_", "HB_", "VA_", "VB_", "LA", "LB"]
+for _n in PS:
+    _buf(_n, 512, F32, "psum")
+NDMA = 24
+SEMAPHORES = ["sV", "sS", "sT", "sG", "loc"] + ["dm%d" % k for k in range(NDMA)] + ["rq%d" % t for t in range(RO)] + ["rp%d" % t for t in range(RO)]
+
+
+def rank_program(g, core, T, topo):
+    rank = T.rank_of(core)
+    if rank is None:
+        return
+    n_ranks = len(T.cores)
+    QS = {"V": g.vector, "S": g.scalar, "T": g.tensor, "G": g, "Y": g.sync}
+    cnt = {q: 0 for q in QS}
+    clk = {q: {} for q in QS}
+    snap, hist, bank, extra = {}, {}, {}, {}
+    ndma = [0]
+
+    def R(n, a=0, b=None, s=1, ps=None, tag=None):
+        if n in PART:
+            n, o, w = PART[n]
+            a, b = a + o, o + (w if b is None else b)
+        elif b is None: b = SCRATCH[n][1][1]
+        ap = T[n][:, a:b:s] if ps is None else T[n][ps, a:b:s]
+        return ap, [(n, a, b, s, tag)]
+
+    def IX(win, off):
+        return win[0].indirect(off[0]), win[1] + off[1]
+
+    def HBM(ap):
+        return ap, []
+
+    def overlap(x, y):
+        if x[1] >= y[2] or y[1] >= x[2]: return False
+        if x[4] is not None and y[4] is not None and x[4] != y[4]: return False
+        return not (x[3] == y[3] > 1 and (x[1] - y[1]) % x[3])
+
+    def learn(q, ev):
+        c = clk[q]
+        for k, v in list(snap.get(ev, {}).items()) + [ev]:
+            if c.get(k, 0) < v: c[k] = v
+
+    def emit(q, fn, rd, wr, dma=False, count=None):
+        deps = {}
+
+        def dep(ev):
+            if clk[q].get(ev[0], 0) < ev[1] and deps.get(ev[0], 0) < ev[1]: deps[ev[0]] = ev[1]
+        for regs, w in ((rd, False), (wr, True)):
+            for r in regs:
+                if r[0] in PS:
+                    for oq, ev in bank.get(r[0], {}).items():
+                        if oq != q: dep(ev)
+                    continue
+                for ev, oq, odma, ow, reg in hist.get(r[0], []):
+                    if not (w or ow) or not overlap(r, reg): continue
+                    if not ow and oq == q and not dma and not odma: continue
+                    dep(ev)
+        evs = list(deps.items())
+        for ev in evs:
+            if any(o != ev and snap.get(o, {}).get(ev[0], 0) >= ev[1] for o in evs): continue
+            QS[q].wait_ge(T.sem[ev[0] if ev[0] not in QS else "s" + ev[0]], ev[1])
+        for ev in evs: learn(q, ev)
+        ins = fn()
+        if count is not None:
+            return
+        if dma:
+            name = "dm%d" % ndma[0]
+            ndma[0] += 1
+            ins.then_inc(T.sem[name], 16)
+            ev = (name, 16)
+        else:
+            cnt[q] += 1
+            ins.then_inc(T.sem["s" + q], 1)
+            ev = (q, cnt[q])
+        snap[ev] = dict(clk[q])
+        for regs, w in ((rd, False), (wr, True)):
+            for r in regs:
+                if r[0] in PS:
+                    bank.setdefault(r[0], {})[q] = ev
+                    continue
+                h = hist.setdefault(r[0], [])
+                if w and r[4] is None and r[3] == 1:
+                    h[:] = [x for x in h if not (r[1] <= x[4][1] and x[4][2] <= r[2])]
+                elif not w:
+                    h[:] = [x for x in h if not (x[1] == q and not dma and not x[2] and not x[3] and x[4] == r)]
+                h.append((ev, q, dma, w, r))
+
+    def landed(name, sem, n):
+        r = R(name)[1][0]
+        hist.setdefault(r[0], []).append(((sem, n), "net", True, True, r))
+
+    def tt(o, x, y, op): emit("V", lambda: g.vector.tensor_tensor(o[0], x[0], y[0], op), x[1] + y[1], o[1])
+
+    def ts(o, x, s1, op, s2=None, op1=None):
+        rd, c = list(x[1]), []
+        for s in (s1, s2):
+            if isinstance(s, tuple):
+                rd += s[1]
+                c.append(s[0])
+            else: c.append(s)
+        if op1 is None: emit("V", lambda: g.vector.tensor_scalar(o[0], x[0], c[0], None, op), rd, o[1])
+        else: emit("V", lambda: g.vector.tensor_scalar(o[0], x[0], c[0], c[1], op, op1), rd, o[1])
+
+    def cp(o, x): emit("V", lambda: g.vector.tensor_copy(o[0], x[0]), x[1], o[1])
+    def fill(o, v): emit("V", lambda: g.vector.memset(o[0], v), [], o[1])
+    def red(o, x, op): emit("V", lambda: g.vector.tensor_reduce(o[0], x[0], AxisListType.X, op), x[1], o[1])
+
+    def scan(o, x, y, init, op0, op1):
+        rd, i = x[1] + y[1], init
+        if isinstance(init, tuple):
+            rd, i = rd + init[1], init[0]
+        emit("V", lambda: g.vector.tensor_tensor_scan(o[0], x[0], y[0], i, op0, op1), rd, o[1])
+
+    def scatter(win, off, x):
+        emit("V", lambda: g.vector.tensor_copy(win[0].indirect(off[0]), x[0]), x[1] + off[1], win[1])
+
+    def act(o, x, f, bias=None, scale=1.0, acc=None):
+        rd, kw, wr = list(x[1]), {"scale": scale}, list(o[1])
+        for k, v in (("bias", bias), ("scale", scale)):
+            if isinstance(v, tuple):
+                rd += v[1]
+                kw[k] = v[0]
+            elif v is not None: kw[k] = v
+        if acc is not None:
+            wr += acc[1]
+            kw["accum_out"] = acc[0]
+        emit("S", lambda: g.scalar.activation(o[0], x[0], f, **kw), rd, wr)
+
+    def sc(o, x, v): act(o, x, AF.Copy, scale=v)
+    def mm(o, l, r, start, stop): emit("T", lambda: g.tensor.matmul(o[0], l[0], r[0], start, stop), l[1] + r[1], o[1])
+    def dma(q, o, x): emit(q, lambda: QS[q].dma_start(o[0], x[0]), x[1], o[1], dma=True)
+
+    def iota(o, pat, base, cm, small=True):
+        if small: emit("G", lambda: g.iota(o[0], pat, base, cm, allow_small_or_imprecise_dtypes=True), [], o[1])
+        else: emit("G", lambda: g.iota(o[0], pat, base, cm), [], o[1])
+
+    def asel(o, x, pat, op, fillv, base, cm): emit("G", lambda: g.affine_select(o[0], x[0], pat, op, fillv, base, cm), x[1], o[1])
+
+    def wrapmm(out, n, src, first, last):
+        b = PART[src][2] if src in PART else SCRATCH[src][1][1]
+        for i in range(16):
+            mm(out, R(n, 15 - i, 143 - i), R(src, i, b, 16), first and i == 0, last and i == 15)
+
+    dma("Y", R("HS"), HBM(T.hy[:, :]))
+    dma("S", R("VS"), HBM(T.vf[:, :]))
+    dma("Y", R("RQ", 0, TY), HBM(T.rq[:, :]))
+    dma("S", R("SG", 0, TY), HBM(T.sg[:, :]))
+    dma("Y", R("WI"), HBM(T.wd[:, :]))
+    dma("S", R("XS", 0, V), HBM(T.xs[:, :]))
+    dma("Y", R("TH"), HBM(T.th[:, :]))
+
+    iota(R("PI"), [[0, 1]], 0, 1, small=False)
+    fill(R("ON"), 1.0)
+    asel(R("GG"), R("ON"), [[-16, 8], [0, 16]], OP.is_ge, 0.0, 0, 1)
+    asel(R("GG"), R("GG"), [[16, 8], [0, 16]], OP.is_ge, 0.0, 15, -1)
+    fill(R("ST"), 0.0)
+    ts(R("PA"), R("PI"), 15, OP.bitwise_and)
+    cp(R("PC"), R("PA"))
+    ts(R("PC1"), R("PC"), 1.0, OP.add)
+    iota(R("CMI"), [[0, 8], [1, 16]], 0, 0)
+    iota(R("BR"), [[1, NB]], 0, 0)
+    iota(R("ER", 0, 96), [[16, 96]], 2560, 0)
+    iota(R("ER", 96, NB), [[32, 64]], 4096, 0)
+    iota(R("YI0"), [[1, 64]], 0, 64, small=False)
+    iota(R("JR"), [[1, 512]], 0, 0)
+    asel(R("ID"), R("ON"), [[-1, 128]], OP.is_equal, 0.0, 0, 1)
+    asel(R("US"), R("GG"), [[1, 128]], OP.is_gt, 0.0, 0, -1)
+    iota(R("M64"), [[1, 16], [0, 4]], 0, 0)
+    iota(R("M16"), [[1, 16]], 0, 0)
+    iota(R("XR0", LN, 576), [[1, 64]], 2560, 0)
+    ts(R("RI"), R("CMI", 0, 16), R("PC"), OP.is_equal)
+
+    def ri(p): return R("RI", p, p + 1)
+    def co(k): return R("CO", k, k + 1)
+
+    def role(k, pairs):
+        for j, (p, v) in enumerate(pairs):
+            if j: ts(co(k), ri(p), float(v), OP.mult, co(k), OP.add)
+            else: ts(co(k), ri(p), float(v), OP.mult)
+
+    ts(R("HXA"), R("HS"), 5, OP.arith_shift_right)
+    cp(R("HB3", 0, 128), R("HXA"))
+    ts(R("HXB"), R("HS"), 31, OP.bitwise_and)
+    cp(R("HB3", 128, 256), R("HXB"))
+    cp(R("HB3", 256, 384), R("VS"))
+    for k, q in ((2, "S"), (0, "Y"), (1, "S")):
+        dma(q, R("ST", 0, V, ps=slice(k, 128, 16), tag=k), R("HB3", 128 * k, 128 * k + 128))
+    cp(R("GM"), R("GG", 0, 128, 16))
+    ts(R("CMJ"), R("CMI"), 1.0, OP.add)
+    tt(R("GK"), R("GG"), R("CMJ"), OP.mult)
+    ts(R("GR2"), R("GK"), ri(2), OP.mult)
+    for i in range(16): ts(R("WV", 128 * i, 128 * i + 128), R("GR2"), float(i + 1), OP.is_ge)
+    ts(R("GR3"), R("GK"), ri(15), OP.mult)
+    for i in range(16): ts(R("PWM", 128 * i, 128 * i + 128), R("GR3"), float(i + 2), OP.is_ge)
+    sc(R("LT"), R("GG"), ri(15))
+    fill(R("Z"), 0.0)
+    cp(R("Z", 15, 143, 16), R("GM"))
+    ts(R("ST", V, STW), R("ST", V, STW), ri(3), OP.add)
+    fill(R("ZR"), 0.0)
+    fill(R("FB", 0, LN), 0.0)
+    ts(R("PIN", 128, NB), R("ZR", 0, 32), R("PC1"), OP.add)
+    sc(R("Z0"), R("Z"), ri(0))
+    sc(R("Z016"), R("Z0"), 16.0)
+    role(1, [(0, 32), (1, 1), (3, 1024)])
+    sc(R("ZY"), R("Z"), co(1))
+    role(5, [(0, 16)])
+    sc(R("G016"), R("GG"), co(5))
+    fill(R("SG", TY, 1040), 0.0)
+    fill(R("RQ", TY, 1040), TY)
+    fill(R("XS", V, XSW), 0.0)
+    fill(R("GTB"), 0.0)
+    ts(R("GTB"), R("GTB"), ri(4), OP.add)
+    ts(R("YJ"), R("YI0"), TY - 1, OP.bitwise_and)
+    tt(R("Y2"), R("YJ"), R("YJ"), OP.mult)
+    ts(R("Y3"), R("Y2"), 4, OP.arith_shift_right)
+    ts(R("Y4"), R("YJ"), 5.0, OP.mult)
+    tt(R("Y5"), R("Y3"), R("Y4"), OP.add)
+    ts(R("Y6"), R("Y5"), 5, OP.arith_shift_right, 31, OP.bitwise_and)
+    cp(R("YD", 0, 64), R("Y6"))
+    ts(R("Y2"), R("Y5"), 31, OP.bitwise_and)
+    cp(R("YD", 64, 128), R("Y2"))
+    for k in range(2):
+        dma("Y", R("GTB", 0, TY, ps=slice(k, 128, 16), tag=k), R("YD", 64 * k, 64 * k + 64))
+
+    def consts2():
+        sc(R("ZM"), R("Z"), -1.0)
+        sc(R("Z2"), R("Z"), 2.0)
+        sc(R("I8"), R("ID"), 8192.0)
+        sc(R("I8N"), R("ID"), -8192.0)
+        sc(R("G32"), R("GG"), 32.0)
+        sc(R("GN"), R("GG"), -1.0)
+        fill(R("RS"), 0.0)
+        for k, v in ((0, 1.0), (1, 32.0), (2, -1.0)): ts(R("RS", k, 128, 16), R("GM"), v, OP.mult)
+        sc(R("RS32"), R("RS"), 32.0)
+        sc(R("RSN"), R("RS"), -1.0)
+        for n in ("YR", "GR"): fill(R(n), 0.0)
+        role(8, [(0, 1024), (1, 32)])
+        role(9, [(0, 32768), (1, 1024)])
+        for k, c in ((0, 8), (1, 9)): ts(R("YR", k, 128, 16), R("GM"), co(c), OP.mult)
+        sc(R("YRN"), R("YR"), -1.0)
+        ts(R("YR", 3, 128, 16), R("GM"), ri(3), OP.mult, 1024.0, OP.mult)
+        role(12, [(0, 1024), (1, 32), (4, 31)])
+        role(13, [(0, 32768), (1, 1024), (4, 992)])
+        role(15, [(4, 1624)])
+        for k, c in ((0, 12), (1, 13), (2, 15)): ts(R("GR", k, 128, 16), R("GM"), co(c), OP.mult)
+        ts(co(14), R("PC"), 2.5, OP.is_gt, 1.0e9, OP.mult)
+        for p, v in ((0, 100), (1, 3200), (2, -0.5)): ts(co(14), ri(p), float(v), OP.mult, co(14), OP.add)
+        for k in range(4):
+            ts(R("DG", 16 * k, 16 * k + 16), R("CMI", 0, 16), R("PC"), OP.is_equal)
+            ts(R("RB", k, k + 1), R("PC"), 16.0 * k + 0.5, OP.add)
+            ts(R("RC", k, k + 1), R("PC"), 16.0 * k, OP.add)
+        for n in ("WF", "KF", "O0", "FF"): fill(R(n, LN, 576), 0.0)
+        ts(R("LB0"), R("TH"), 8192.0, OP.add)
+        cp(R("LM"), R("LB0"))
+
+    def consts3():
+        fill(R("WD", V, WDW), 0.0)
+        fill(R("WD", MARK, MARK + 1), -1.0)
+        fill(R("SVB"), 0.0)
+        sc(R("Z32"), R("Z"), 32.0)
+        sc(R("ZM16"), R("Z"), -16.0)
+        ts(co(6), R("PC"), 10.0, OP.mult, 1.0, OP.add)
+        sc(R("ZU"), R("Z"), co(6))
+        role(7, [(2, -131072)])
+        sc(R("ZV"), R("Z"), co(7))
+        fill(R("RF"), 0.0)
+        for k, v in ((0, 32.0), (1, 1024.0)): ts(R("RF", k, 128, 16), R("GM"), v, OP.mult)
+        sc(R("GF"), R("GG"), 1.0)
+        sc(R("SF"), R("ON"), ri(0))
+        sc(R("PL"), R("US"), 2.0)
+        tt(R("PL"), R("PL"), R("ID"), OP.subtract)
+        role(11, [(0, 32), (1, 1)])
+        ts(R("YHM"), R("GM"), co(11), OP.mult)
+        ts(R("RE", 0, 1), R("PC"), 1.0 - 10000.0, OP.add)
+        ts(R("RE", 1, 2), R("PC"), 17.0 - 10000.0, OP.add)
+        for k in range(2): ts(R("TR", 32 * k, 32 * k + 32), R("JR", 0, 32), R("RC", k, k + 1), OP.is_lt)
+
+    def lanes(t):
+        c = (ST0 * t) % V
+        b0 = c // 16
+        for i in range(16):
+            mm(R("LA", 0, 128), R("WV", 128 * i, 128 * i + 128), R("ST", i, V, 16), i == 0, i == 15)
+        if t: request(t - 1)
+        ts(R("PIN", 0, 128 - b0), R("LA", b0, 128), -1.0, OP.mult, R("PC1"), OP.add)
+        if b0: ts(R("PIN", 128 - b0, 128), R("LA", 0, b0), -1.0, OP.mult, R("PC1"), OP.add)
+        mm(R("LB", 0, NB), R("LT"), R("PIN"), True, True)
+        for i in range(16):
+            mm(R("LA", 0, 10), R("PWM", 128 * i, 128 * i + 128), R("PIN", i, NB, 16), i == 0, False)
+        ts(R("EM"), R("LB", 0, NB), 0.0, OP.is_equal)
+        tt(R("EMC"), R("EM"), R("ER"), OP.mult)
+        scan(R("BPI"), R("LB", 0, NB), R("ZR"), 0.0, OP.add, OP.max)
+        wrapmm(R("LA", 0, 10), "Z0", "EMC", False, True)
+        tt(R("BPX"), R("BPI"), R("LB", 0, NB), OP.subtract)
+        tt(R("OFF"), R("LA", 0, 10), R("BPX", 0, NB, 16), OP.add)
+        cp(R("OF16"), R("OFF"))
+        tt(R("PW"), R("BPX"), R("PIN"), OP.add)
+        scatter(R("FB"), R("OF16"), R("BR"))
+        scan(R("FR"), R("FB", 0, LN), R("FB", 0, LN), 0.0, OP.max, OP.max)
+        wrapmm(R("LB", 0, 32), "Z0", "FR", True, True)
+        wrapmm(R("LA", 0, 32), "Z016", "FR", True, False)
+        cp(R("FL16"), R("LB", 0, 32))
+        tt(R("E"), IX(R("PW"), R("FL16")), R("JR"), OP.is_le)
+        if c:
+            ts(R("A1"), R("LB", 0, 32), float(128 - b0), OP.is_ge, -2048.0, OP.mult)
+            ts(R("A2"), R("LB", 0, 32), 128.0, OP.is_ge, float(2048 - c), OP.mult)
+            tt(R("AJ0"), R("A1"), R("A2"), OP.add)
+            mm(R("LA", 0, 32), R("ID"), R("AJ0"), False, False)
+        wrapmm(R("LA", 0, 32), "Z", "E", False, True)
+        ts(R("A16"), R("LA", 0, 32), float(c), OP.add)
+        if t: service0(t - 1)
+        cp(R("YG"), IX(R("ST"), R("A16")))
+        wrapmm(R("LB", 0, 32), "ZY", "YG", True, True)
+        mm(R("VA_"), R("G016"), R("FR"), True, False)
+        mm(R("VA_"), R("GG"), R("E"), False, True)
+        if t: service1(t - 1)
+        act(R("XR0", 0, LN), R("VA_"), AF.Copy)
+        fill(R("FB", 0, LN), 0.0)
+
+    def types(k):
+        a, b = k * CW, k * CW + CW
+        cp(R("KF", a, b), IX(R("RQ"), R("Y16", a // 16, b // 16)))
+        cp(R("K16", a, b), R("KF", a, b))
+
+    def typed(k):
+        types(k)
+        sgather(k)
+
+    def words(k):
+        a, b = k * CW, k * CW + CW
+        cp(R("WF", a, b), IX(R("WD"), R("A16", a // 16, b // 16)))
+        cp(R("W16", a, b), R("WF", a, b))
+
+    def dbank(k): return R("DB_" if k % 2 else "DA_", 0, CW)
+    def hbank(k, j): return R("HB_" if k % 2 else "HA_", j * CW, j * CW + CW)
+
+    def sgather(k):
+        act(R("B%d" % k), IX(R("SG"), R("K16", k * CW, k * CW + CW)), AF.Copy)
+
+    def hgather(k):
+        act(R("H%d" % (k % 2)), IX(R("ST"), R("W16", k * CW, k * CW + CW)), AF.Copy)
+
+    def diff(k):
+        tt(R("D%d" % (k % 2)), IX(R("XS"), R("W16", k * CW, k * CW + CW)), R("B%d" % k), OP.subtract)
+
+    def dsum1(k): wrapmm(dbank(k), "ZM", "D%d" % (k % 2), True, False)
+
+    def dsum2(k):
+        ts(R("R%d" % (k % 2)), R("D%d" % (k % 2)), 0.0, OP.max)
+        wrapmm(dbank(k), "Z2", "R%d" % (k % 2), False, False)
+
+    def other(k):
+        a, b = k * CW, k * CW + CW
+        wrapmm(hbank(k, 0), "ZY", "H%d" % (k % 2), True, True)
+        tt(R("O0", a, b), hbank(k, 0), R("KF", a, b), OP.not_equal)
+        mm(dbank(k), R("I8N"), R("DA", a, b), False, False)
+        mm(dbank(k), R("I8"), R("O0", a, b), False, True)
+
+    def verdict1(k):
+        ts(R("FF", k * CW, k * CW + CW), dbank(k), R("LM"), OP.is_gt)
+
+    def verdict2(k):
+        a, b = k * CW, k * CW + CW
+        hx = hbank(k, 1)
+        for o, (m32, mn, m1) in ((R("VA_", a, b), ("G32", "GN", "GG")), (R("VB_", a, b), ("RS32", "RSN", "RS")), (hx, ("RS32", "RSN", "RS"))):
+            mm(o, R(mn), R("O0", a, b), True, False)
+            mm(o, R(m1), R("DA", a, b), False, False)
+            mm(o, R(m32), R("FF", a, b), False, o is not hx)
+        mm(hx, R("GR"), R("GB", a, b), False, False)
+        mm(hx, R("YRN"), R("YG", a, b), False, True)
+        mm(hbank(k, 2), R("YR"), R("YG", a, b), True, True)
+
+    def outcome(k):
+        a, b = k * CW, k * CW + CW
+        ts(R("PM", a, b), R("VA_", a, b), 0.0, OP.is_lt)
+        scan(R("PP", a, b), R("PM", a, b), R("PM", a, b), R("PP", a - 1, a) if k else 0.0, OP.add, OP.max)
+        ts(R("MU", a, b), R("VB_", a, b), co(14), OP.is_gt)
+        tt(R("T2", a, b), hbank(k, 1), R("MU", a, b), OP.mult)
+        tt(R("QQ", a, b), hbank(k, 2), R("T2", a, b), OP.add)
+        ts(R("DD", a, b), R("QQ", a, b), 10, OP.arith_shift_right, 31, OP.bitwise_and)
+
+    def count_lists():
+        for k in range(2):
+            act(R("JK"), R("PP"), AF.Sign, bias=R("RB", k, k + 1), scale=-1.0, acc=R("AC", k, k + 1))
+        act(R("NG"), R("VA_"), AF.Sign, bias=-0.5, acc=R("AC", 6, 7))
+        act(R("MN"), R("VA_"), AF.Sign, bias=-100.0)
+
+    def repair_scan():
+        scan(R("RP"), R("NG"), R("MN"), 0.0, OP.add, OP.subtract)
+        for k in range(4):
+            act(R("JK"), R("RP"), AF.Sign, bias=R("RB", k, k + 1), scale=-0.5, acc=R("AC", 2 + k, 3 + k))
+
+    def retypes():
+        ts(R("PL16"), R("AC", 0, 2), 0.5, OP.mult, 256.0, OP.add)
+        cp(R("OG"), IX(R("O0"), R("PL16")))
+        cp(R("KG"), IX(R("KF"), R("PL16")))
+        cp(R("WG"), IX(R("WF"), R("PL16")))
+        ts(R("KL"), R("KG"), float(TY), OP.is_lt)
+        tt(R("OR"), R("OG"), R("KL"), OP.mult)
+        mm(R("LA", 0, 32), R("PL"), R("OR"), True, True)
+        ts(R("WG"), R("WG"), float(-DUMP), OP.add)
+        ts(R("FI"), R("LA", 0, 32), 0.0, OP.is_lt)
+        tt(R("WK"), R("WG"), R("FI"), OP.mult)
+        tt(R("KK"), R("KG"), R("FI"), OP.mult)
+        mm(R("LA", 0, 32), R("GF"), R("WK"), True, True)
+        mm(R("LB", 0, 32), R("RF"), R("KK"), True, True)
+        tt(R("WDG"), R("LA", 0, 32), R("DG", 0, 32), OP.mult)
+        for k in range(2): red(R("W2", k, k + 1), R("WDG", 16 * k, 16 * k + 16), OP.add)
+        for k in range(2): ts(R("EQ1", 32 * k, 32 * k + 32), R("LA", 0, 32), R("W2", k, k + 1), OP.is_equal)
+        tt(R("EQ2"), R("EQ1"), R("TR"), OP.mult)
+        cp(R("KI1"), R("LB", 0, 32))
+        for k in range(2): red(R("DU", k, k + 1), R("EQ2", 32 * k, 32 * k + 32), OP.max)
+        ts(R("KD"), R("KI1"), 10, OP.arith_shift_right, 31, OP.bitwise_and)
+        ts(R("DE"), R("DU"), 10000.0, OP.mult)
+        tt(R("DE2"), R("DE"), R("RE"), OP.add)
+        tt(R("OX"), R("W2"), R("DE2"), OP.max)
+        ts(R("OX16"), R("OX"), float(DUMP), OP.add)
+        scatter(R("ST"), R("OX16"), R("KD"))
+
+    def count_good():
+        ts(R("GC1"), R("AC", 6, 7), -0.5, OP.mult, 256.0, OP.add)
+        tt(R("GS"), R("GC1"), R("GP"), OP.subtract)
+        mm(R("LB", 0, 1), R("SF"), R("GS"), True, True)
+        cp(R("BI1"), R("LB", 0, 1))
+        ts(R("BJ"), R("BI1"), 255, OP.bitwise_and)
+        tt(R("LM"), R("LB0"), R("BJ"), OP.add)
+
+    def send(buf, land, dst, sem):
+        eng = topo.engines(core, dst)[:8]
+        mask = sum(1 << e for e in eng)
+        rid, pid, _ = topo.addr(dst)
+        x, y = R(buf), R(land)
+        emit("G", lambda: g.remote_dma(y[0], x[0], T.sem[sem], T.sem.loc, pid, rid, mask), x[1], [], count=len(eng))
+        extra["loc"] = extra.get("loc", 0) + len(eng)
+
+    def helper(t): return T.cores[(rank + 1 + t % (n_ranks - 1)) % n_ranks]
+    def asker(t): return T.cores[(rank - 1 - t % (n_ranks - 1)) % n_ranks]
+
+    def request(t):
+        c = (ST0 * t) % V
+        ts(R("RN1"), R("AC", 2, 6), 0.5, OP.mult, 256.0, OP.add)
+        ts(R("RM"), R("RN1"), float(LN), OP.is_ge)
+        tt(R("RK"), R("RM"), R("RC"), OP.mult)
+        tt(R("RL"), R("RN1"), R("RK"), OP.add)
+        cp(R("RL16"), R("RL"))
+        cp(R("XG1"), IX(R("XR0"), R("RL16")))
+        tt(R("XD"), R("XG1"), R("DG"), OP.mult)
+        for k in range(4): red(R("RX", k, k + 1), R("XD", 16 * k, 16 * k + 16), OP.add)
+        if c:
+            ts(R("X1"), R("RX"), float(2048 - c), OP.is_ge, -2048.0, OP.mult)
+            ts(R("X2"), R("RX"), 2048.0, OP.is_ge, float(2048 - c), OP.mult)
+            tt(R("X3"), R("RX"), R("X1"), OP.add)
+            tt(R("X5"), R("X3"), R("X2"), OP.add)
+            ts(R("RA16"), R("X5"), float(c), OP.add)
+        else:
+            cp(R("RA16"), R("RX"))
+        cp(R("XQ%d" % t), IX(R("XS"), R("RA16")))
+        send("XQ%d" % t, "QX%d" % t, helper(t), "rq%d" % t)
+
+    def service0(t):
+        X = "QX%d" % t
+        landed(X, "rq%d" % t, len(topo.engines(asker(t), core)[:8]))
+        wrapmm(R("HA_", 0, 4), "ZU", X, True, True)
+
+    def service1(t):
+        cp(R("UI1"), R("HA_", 0, 4))
+        ts(R("UA"), R("UI1"), V - 1, OP.bitwise_and)
+        tt(R("UU"), R("UA"), R("UA"), OP.mult)
+        ts(R("TM"), R("UA"), 2.0, OP.mult, 1.0, OP.add)
+        ts(R("UV"), R("UU"), 5, OP.arith_shift_right)
+        tt(R("BS1"), R("UV"), R("UA"), OP.add)
+        for k in range(4):
+            ts(R("CI1", k, 64, 4), R("M16"), R("TM", k, k + 1), OP.mult, R("BS1", k, k + 1), OP.add)
+        ts(R("CA"), R("CI1"), V - 1, OP.bitwise_and)
+        cp(R("C16"), R("CA"))
+        act(R("VG"), IX(R("SVB"), R("C16")), AF.Copy)
+
+    def service2(t, a=0, b=16):
+        X = "QX%d" % t
+        for m in range(a, b):
+            tt(R("DX", 64 * m, 64 * m + 64), IX(R("XS"), R("C16", 4 * m, 4 * m + 4)), R(X), OP.subtract)
+        if b == 16:
+            ts(R("RX2"), R("DX"), 0.0, OP.max)
+            wrapmm(R("LB", 0, 64), "ZV", "VG", True, False)
+            wrapmm(R("LB", 0, 64), "ZM16", "DX", False, False)
+            wrapmm(R("LB", 0, 64), "Z32", "RX2", False, True)
+
+    def service3(t):
+        tt(R("KEY"), R("LB", 0, 64), R("M64"), OP.add)
+        for k in range(4): red(R("KM1", k, k + 1), R("KEY", k, 64, 4), OP.min)
+        cp(R("MI"), R("KM1"))
+        ts(R("NN"), R("KM1"), 0.0, OP.is_ge, 4096.0, OP.mult)
+        ts(R("MJ"), R("MI"), 15, OP.bitwise_and)
+        tt(R("P1"), R("MJ"), R("TM"), OP.mult)
+        tt(R("P2"), R("P1"), R("BS1"), OP.add)
+        ts(R("P3"), R("P2"), V - 1, OP.bitwise_and)
+        tt(R("P4"), R("P3"), R("NN"), OP.add)
+        ts(R("BB16"), R("P4"), float(MARK), OP.min)
+        cp(R("WR%d" % t), IX(R("WD"), R("BB16")))
+        send("WR%d" % t, "QW%d" % t, asker(t), "rp%d" % t)
+
+    def merge(t):
+        W = "QW%d" % t
+        cp(R("WO1"), IX(R("WD"), R("RA16")))
+        cp(R("FLG"), IX(R("FF"), R("RL16")))
+        landed(W, "rp%d" % t, len(topo.engines(helper(t), core)[:8]))
+        ts(R("MK"), R(W), 0.0, OP.is_ge)
+        tt(R("DW"), R(W), R("WO1"), OP.subtract)
+        tt(R("FM"), R("MK"), R("FLG"), OP.mult)
+        tt(R("DM"), R("DW"), R("FM"), OP.mult)
+        win, off, x, y = R("WD"), R("RA16"), R("WO1"), R("DM")
+        emit("V", lambda: g.vector.tensor_tensor(win[0].indirect(off[0]), x[0], y[0], OP.add), x[1] + y[1] + off[1], win[1])
+
+    for t in range(RO):
+        if t == 0: consts2()
+        lanes(t)
+        if t: service2(t - 1, 0, 6)
+        cp(R("Y16"), R("LB", 0, 32))
+        for k in range(TF[0]): typed(k)
+        if t: service2(t - 1, 6, 16)
+        for k in range(TF[0], TF[1]): typed(k)
+        if t == 0:
+            consts3()
+            cp(R("WD", 0, V), R("WI"))
+        else:
+            service3(t - 1)
+        for k in range(TF[1], NCH): types(k)
+        ts(R("DA"), R("K16"), float(TY), OP.is_equal)
+        dma("Y", R("SVB", 0, V, ps=slice(2, 128, 16)), R("ST", 0, V, ps=slice(2, 128, 16)))
+        if t: count_good()
+        ts(R("GP"), R("BPI", 127, 128), -1.0, OP.mult, float(LN), OP.add)
+        ts(R("GP"), R("GP"), 0.0, OP.max)
+        act(R("GB"), IX(R("GTB"), R("Y16")), AF.Copy)
+        if t: merge(t - 1)
+        for k in range(TF[1], SB): sgather(k)
+        for k in range(NCH + 1):
+            if k < NCH:
+                words(k)
+                hgather(k)
+                if k + SB < NCH: sgather(k + SB)
+                diff(k)
+            if k: other(k - 1)
+            if k < NCH: dsum1(k)
+            if k > 1: outcome(k - 2)
+            if k: verdict1(k - 1)
+            if k < NCH: dsum2(k)
+            if k: verdict2(k - 1)
+        outcome(NCH - 1)
+        count_lists()
+        if t == RO - 1:
+            repair_scan()
+            request(t)
+        scatter(R("ST"), R("A16"), R("DD"))
+        if t < RO - 1: repair_scan()
+        retypes()
+    service0(RO - 1)
+    service1(RO - 1)
+    service2(RO - 1)
+    service3(RO - 1)
+    for k in range(4):
+        mm(R(PS[k], 0, 512, ps=slice(0, 8)), R("YHM"), R("ST", 512 * k, 512 * k + 512), True, True)
+        act(R("YO", 512 * k, 512 * k + 512, ps=slice(0, 8)), R(PS[k], 0, 512, ps=slice(0, 8)), AF.Copy)
+    dma("Y", HBM(T.yh[:, :]), R("YO", 0, V, ps=slice(0, 8)))
+    dma("G", HBM(T.yv[:, :]), R("ST", 0, V, ps=slice(2, 128, 16)))
+    merge(RO - 1)
+    dma("Y", HBM(T.ym[:, :]), R("WD", 0, V))
+    for q in ("V", "S", "T", "G"):
+        g.wait_ge(T.sem["s" + q], cnt[q])
+    for k in range(ndma[0]): g.wait_ge(T.sem["dm%d" % k], 16)
+    g.wait_ge(T.sem.loc, extra["loc"])

@@ -8,10 +8,14 @@ DUMP = 2688
 MARK = 2736
 WDW = 2752
 XSW = 2640
-NCH = 4
+NCH = 8
 CW = LN // NCH
-TF = (1, 2)
-SB = 2
+NBF = 4
+TF = (2, 4)
+SB = 4
+PARTS = (0, 384, 512)
+CY, GAT, SCA, PEC, WK, LOOK = 0.83e-3, 1.5, 3.0, 0.5e-3, 0.1, 0.0
+KB, GBK, UB, NBK = "DA_", "DB_", "HA_", ("LA", "LB", "VB_")
 
 BFB, F32, I32, U16 = "bfloat16", "float32", "int32", "uint16"
 SCRATCH = {}
@@ -34,9 +38,8 @@ for _n, _c, _d in [
     ("FR", 512, BFB), ("FL16", 32, U16), ("AJ", 96, BFB), ("E", 512, BFB), ("A16", 32, U16),
     ("XR0", 576, F32), ("YG", 512, BFB), ("Y16", 32, U16), ("GB", 512, BFB),
     ("KF", 576, F32), ("K16", 512, U16), ("DA", 512, BFB), ("WF", 576, F32), ("W16", 512, U16), ("LIM", 2, F32),
-    ("H0", 16 * CW, BFB), ("H1", 16 * CW, BFB), ("D0", 16 * CW, BFB), ("D1", 16 * CW, BFB), ("R0", 16 * CW, BFB), ("R1", 16 * CW, BFB),
     ("O0", 576, BFB), ("FF", 576, BFB), ("PM", 512, BFB), ("PP", 512, BFB), ("MU", 512, BFB), ("T2", 512, F32), ("QQ", 512, I32), ("DD", 512, I32),
-    ("NG", 512, BFB), ("MN", 512, BFB), ("RP", 512, BFB), ("JK", 512, BFB), ("AC", 8, F32),
+    ("NG", 512, BFB), ("MN", 512, BFB), ("RP", 512, BFB), ("JK", 3072, BFB), ("AC", 24, F32),
     ("PL16", 2, U16), ("WKG", 160, F32), ("OKR", 96, BFB), ("FI", 32, F32),
     ("WW", 10, F32), ("EQ", 128, F32), ("OX16", 2, U16), ("KI", 64, I32), ("GC", 3, F32), ("BI", 2, I32),
     ("RN", 20, F32), ("RL16", 4, U16), ("XG", 128, F32), ("X4", 16, F32), ("RA16", 4, U16),
@@ -44,7 +47,8 @@ for _n, _c, _d in [
     ("KEY", 64, F32), ("KM", 16, F32), ("BB16", 4, U16), ("FLG", 64, BFB), ("WO", 320, F32), ("YO", V, F32),
 ]:
     _buf(_n, _c, _d)
-for _k in range(NCH): _buf("B%d" % _k, 16 * CW, BFB)
+_CHK = ["B%d" % k for k in range(NCH)] + [c + "%d" % k for c in "HDR" for k in range(NBF)]
+for _n in _CHK: _buf(_n, 16 * CW, BFB)
 for _t in range(RO):
     _buf("XQ%d" % _t, SL, BFB)
     _buf("QX%d" % _t, SL, BFB)
@@ -81,7 +85,7 @@ def _pack(name, parts):
 
 _pack("REQ", ["XQ%d" % t for t in range(RO)] + ["QX%d" % t for t in range(RO)])
 _pack("REP", ["WR%d" % t for t in range(RO)] + ["QW%d" % t for t in range(RO)])
-_pack("CHK", ["B%d" % k for k in range(NCH)] + ["H0", "H1", "D0", "D1", "R0", "R1"])
+_pack("CHK", _CHK)
 _pack("CF", ["JR", "ZR", "DG", "TR", "M64", "M16", "RI", "CO", "RB", "RC", "RE", "PC", "PC1"])
 _pack("CB", ["BR", "ER", "CMI", "CMJ", "GK", "GG", "ID", "ON"])
 PS = ["DA_", "DB_", "HA_", "HB_", "VA_", "VB_", "LA", "LB"]
@@ -126,7 +130,70 @@ def rank_program(g, core, T, topo):
         for k, v in list(snap.get(ev, {}).items()) + [ev]:
             if c.get(k, 0) < v: c[k] = v
 
-    def emit(q, fn, rd, wr, dma=False, count=None):
+    nodes, sent = [], {}
+
+    def emit(q, fn, rd, wr, cost, dma=False, count=None, then=0.0, before=()):
+        nodes.append([q, [(fn, rd, wr, dma, count)], rd, wr, cost, then, before])
+        return len(nodes) - 1
+
+    def schedule():
+        n = len(nodes)
+        succ, npred = [[] for _ in range(n)], [0] * n
+        last, seen = {}, {}
+        for i, (q, calls, rd, wr, cost, then, before) in enumerate(nodes):
+            pred = {b: True for b in before}
+            for regs, w in ((rd, False), (wr, True)):
+                for r in regs:
+                    if r[0] in PS:
+                        for j, oq, ow in last.get(r[0], []):
+                            if j != i and (w or ow or oq != q): pred[j] = pred.get(j, False) or oq != q
+                    else:
+                        for j, ow, reg in seen.get(r[0], []):
+                            if j != i and (w or ow) and overlap(r, reg): pred[j] = True
+            for regs, w in ((rd, False), (wr, True)):
+                for r in regs:
+                    if r[0] in PS:
+                        h = last.setdefault(r[0], [])
+                        if w: h[:] = [x for x in h if x[0] == i]
+                        h.append((i, q, w))
+                    else:
+                        h = seen.setdefault(r[0], [])
+                        if w and r[4] is None and r[3] == 1: h[:] = [x for x in h if x[0] == i or not (r[1] <= x[2][1] and x[2][2] <= r[2])]
+                        h.append((i, w, r))
+            npred[i] = len(pred)
+            for j, wait in pred.items(): succ[j].append((i, wait))
+        far = [0.0] * n
+        for i in range(n - 1, -1, -1):
+            far[i] = nodes[i][4] + nodes[i][5] + max([far[j] + (WK if w else 0.0) for j, w in succ[i]] or [0.0])
+        ready, free, order, left = {}, {}, [], n
+        at = [0.0] * n
+        for i in range(n):
+            if npred[i] == 0: ready.setdefault(nodes[i][0], []).append(i)
+        while left:
+            best = None
+            for q, l in ready.items():
+                if not l: continue
+                f = free.get(q, 0.0)
+                t0 = max(f, min(at[i] for i in l))
+                i = max((i for i in l if at[i] <= t0 + LOOK), key=lambda i: (far[i] - max(0.0, at[i] - t0), -i))
+                t1 = max(f, at[i])
+                if best is None or t1 < best[0]: best = (t1, i, q)
+            t1, i, q = best
+            ready[q].remove(i)
+            order.append((t1, i))
+            left -= 1
+            if q != "N": free[q] = t1 + nodes[i][4]
+            for j, w in succ[i]:
+                at[j] = max(at[j], t1 + nodes[i][4] + (nodes[i][5] + WK if w else 0.0))
+                npred[j] -= 1
+                if npred[j] == 0: ready.setdefault(nodes[j][0], []).append(j)
+        for _, i in order:
+            q, calls = nodes[i][0], nodes[i][1]
+            for fn, rd, wr, dma, count in calls:
+                if q == "N": fn()
+                else: issue(q, fn, rd, wr, dma, count)
+
+    def issue(q, fn, rd, wr, dma=False, count=None):
         deps = {}
 
         def dep(ev):
@@ -139,7 +206,6 @@ def rank_program(g, core, T, topo):
                     continue
                 for ev, oq, odma, ow, reg in hist.get(r[0], []):
                     if not (w or ow) or not overlap(r, reg): continue
-                    if not ow and oq == q and not dma and not odma: continue
                     dep(ev)
         evs = list(deps.items())
         for ev in evs:
@@ -172,10 +238,17 @@ def rank_program(g, core, T, topo):
                 h.append((ev, q, dma, w, r))
 
     def landed(name, sem, n):
-        r = R(name)[1][0]
-        hist.setdefault(r[0], []).append(((sem, n), "net", True, True, r))
+        r = R(name)[1]
+        emit("N", lambda: hist.setdefault(r[0][0], []).append(((sem, n), "net", True, True, r[0])), [], r, 0.1, then=2.0, before=(sent[sem],))
 
-    def tt(o, x, y, op): emit("V", lambda: g.vector.tensor_tensor(o[0], x[0], y[0], op), x[1] + y[1], o[1])
+    def cols(x): return (x[1][-1][2] - x[1][-1][1] + x[1][-1][3] - 1) // x[1][-1][3] * (16 if len(x[1]) > 1 else 1)
+
+    def narrow(*xs): return all(x[1][0][0] not in PS and SCRATCH[x[1][0][0]][2] in (BFB, U16) for x in xs)
+
+    def vc(x, per): return 0.05 + cols(x) * GAT * CY if len(x[1]) > 1 else max(64.0, cols(x) * per) * CY
+
+    def tt(o, x, y, op):
+        emit("V", lambda: g.vector.tensor_tensor(o[0], x[0], y[0], op), x[1] + y[1], o[1], vc(x, 1 if x[1][0][0] in PS or y[1][0][0] in PS else 2))
 
     def ts(o, x, s1, op, s2=None, op1=None):
         rd, c = list(x[1]), []
@@ -184,21 +257,22 @@ def rank_program(g, core, T, topo):
                 rd += s[1]
                 c.append(s[0])
             else: c.append(s)
-        if op1 is None: emit("V", lambda: g.vector.tensor_scalar(o[0], x[0], c[0], None, op), rd, o[1])
-        else: emit("V", lambda: g.vector.tensor_scalar(o[0], x[0], c[0], c[1], op, op1), rd, o[1])
+        w = vc(x, 0.5 if narrow(o, x) else 1)
+        if op1 is None: emit("V", lambda: g.vector.tensor_scalar(o[0], x[0], c[0], None, op), rd, o[1], w)
+        else: emit("V", lambda: g.vector.tensor_scalar(o[0], x[0], c[0], c[1], op, op1), rd, o[1], w)
 
-    def cp(o, x): emit("V", lambda: g.vector.tensor_copy(o[0], x[0]), x[1], o[1])
-    def fill(o, v): emit("V", lambda: g.vector.memset(o[0], v), [], o[1])
-    def red(o, x, op): emit("V", lambda: g.vector.tensor_reduce(o[0], x[0], AxisListType.X, op), x[1], o[1])
+    def cp(o, x): emit("V", lambda: g.vector.tensor_copy(o[0], x[0]), x[1], o[1], vc(x, 0.5 if narrow(o, x) else 1))
+    def fill(o, v): emit("V", lambda: g.vector.memset(o[0], v), [], o[1], vc(o, 0.5 if narrow(o) else 1))
+    def red(o, x, op): emit("V", lambda: g.vector.tensor_reduce(o[0], x[0], AxisListType.X, op), x[1], o[1], vc(x, 1))
 
     def scan(o, x, y, init, op0, op1):
         rd, i = x[1] + y[1], init
         if isinstance(init, tuple):
             rd, i = rd + init[1], init[0]
-        emit("V", lambda: g.vector.tensor_tensor_scan(o[0], x[0], y[0], i, op0, op1), rd, o[1])
+        emit("V", lambda: g.vector.tensor_tensor_scan(o[0], x[0], y[0], i, op0, op1), rd, o[1], vc(x, 0.5 if narrow(o, x, y) else 1))
 
     def scatter(win, off, x):
-        emit("V", lambda: g.vector.tensor_copy(win[0].indirect(off[0]), x[0]), x[1] + off[1], win[1])
+        emit("V", lambda: g.vector.tensor_copy(win[0].indirect(off[0]), x[0]), x[1] + off[1], win[1], 0.05 + cols(x) * SCA * CY)
 
     def act(o, x, f, bias=None, scale=1.0, acc=None):
         rd, kw, wr = list(x[1]), {"scale": scale}, list(o[1])
@@ -210,22 +284,36 @@ def rank_program(g, core, T, topo):
         if acc is not None:
             wr += acc[1]
             kw["accum_out"] = acc[0]
-        emit("S", lambda: g.scalar.activation(o[0], x[0], f, **kw), rd, wr)
+        emit("S", lambda: g.scalar.activation(o[0], x[0], f, **kw), rd, wr, vc(x, 1) + 0.02)
 
     def sc(o, x, v): act(o, x, AF.Copy, scale=v)
-    def mm(o, l, r, start, stop): emit("T", lambda: g.tensor.matmul(o[0], l[0], r[0], start, stop), l[1] + r[1], o[1])
-    def dma(q, o, x): emit(q, lambda: QS[q].dma_start(o[0], x[0]), x[1], o[1], dma=True)
+
+    def mms(o, lrs, first, last):
+        calls, rds, w = [], [], 0.0
+        for k, (l, r) in enumerate(lrs):
+            st, sp = first and k == 0, last and k == len(lrs) - 1
+            calls.append((lambda l=l, r=r, st=st, sp=sp: g.tensor.matmul(o[0], l[0], r[0], st, sp), l[1] + r[1], o[1], False, None))
+            rds += l[1] + r[1]
+            w += max(64, cols(r)) * PEC * (4 if SCRATCH[l[1][0][0]][2] == F32 else 1)
+        nodes.append(["T", calls, rds, o[1], w, 0.0, ()])
+
+    def mm(o, l, r, start, stop): mms(o, [(l, r)], start, stop)
+
+    def dma(q, o, x):
+        w = sum((r[2] - r[1]) * (4 if SCRATCH[r[0]][2] in (F32, I32) else 2) * 128 for r in (o[1] or x[1])[:1]) / 2.0e5
+        emit(q, lambda: QS[q].dma_start(o[0], x[0]), x[1], o[1], 0.1, dma=True, then=2.0 + w)
 
     def iota(o, pat, base, cm, small=True):
-        if small: emit("G", lambda: g.iota(o[0], pat, base, cm, allow_small_or_imprecise_dtypes=True), [], o[1])
-        else: emit("G", lambda: g.iota(o[0], pat, base, cm), [], o[1])
+        w = 0.13 + 2 * cols(o) * CY
+        if small: emit("G", lambda: g.iota(o[0], pat, base, cm, allow_small_or_imprecise_dtypes=True), [], o[1], w)
+        else: emit("G", lambda: g.iota(o[0], pat, base, cm), [], o[1], w)
 
-    def asel(o, x, pat, op, fillv, base, cm): emit("G", lambda: g.affine_select(o[0], x[0], pat, op, fillv, base, cm), x[1], o[1])
+    def asel(o, x, pat, op, fillv, base, cm):
+        emit("G", lambda: g.affine_select(o[0], x[0], pat, op, fillv, base, cm), x[1], o[1], 0.17 + 2 * cols(o) * CY)
 
     def wrapmm(out, n, src, first, last):
         b = PART[src][2] if src in PART else SCRATCH[src][1][1]
-        for i in range(16):
-            mm(out, R(n, 15 - i, 143 - i), R(src, i, b, 16), first and i == 0, last and i == 15)
+        mms(out, [(R(n, 15 - i, 143 - i), R(src, i, b, 16)) for i in range(16)], first, last)
 
     dma("Y", R("HS"), HBM(T.hy[:, :]))
     dma("S", R("VS"), HBM(T.vf[:, :]))
@@ -364,14 +452,12 @@ def rank_program(g, core, T, topo):
     def lanes(t):
         c = (ST0 * t) % V
         b0 = c // 16
-        for i in range(16):
-            mm(R("LA", 0, 128), R("WV", 128 * i, 128 * i + 128), R("ST", i, V, 16), i == 0, i == 15)
+        mms(R("LA", 0, 128), [(R("WV", 128 * i, 128 * i + 128), R("ST", i, V, 16)) for i in range(16)], True, True)
         if t: request(t - 1)
         ts(R("PIN", 0, 128 - b0), R("LA", b0, 128), -1.0, OP.mult, R("PC1"), OP.add)
         if b0: ts(R("PIN", 128 - b0, 128), R("LA", 0, b0), -1.0, OP.mult, R("PC1"), OP.add)
         mm(R("LB", 0, NB), R("LT"), R("PIN"), True, True)
-        for i in range(16):
-            mm(R("LA", 0, 10), R("PWM", 128 * i, 128 * i + 128), R("PIN", i, NB, 16), i == 0, False)
+        mms(R("LA", 0, 10), [(R("PWM", 128 * i, 128 * i + 128), R("PIN", i, NB, 16)) for i in range(16)], True, False)
         ts(R("EM"), R("LB", 0, NB), 0.0, OP.is_equal)
         tt(R("EMC"), R("EM"), R("ER"), OP.mult)
         scan(R("BPI"), R("LB", 0, NB), R("ZR"), 0.0, OP.add, OP.max)
@@ -417,27 +503,28 @@ def rank_program(g, core, T, topo):
         cp(R("W16", a, b), R("WF", a, b))
 
     def dbank(k): return R("DB_" if k % 2 else "DA_", 0, CW)
-    def hbank(k, j): return R("HB_" if k % 2 else "HA_", j * CW, j * CW + CW)
+    def hbank(k): return R("HB_" if k % 2 else "HA_", 0, CW)
+    def nbank(k, j): return R(NBK[k % len(NBK)], j * CW, j * CW + CW)
 
     def sgather(k):
         act(R("B%d" % k), IX(R("SG"), R("K16", k * CW, k * CW + CW)), AF.Copy)
 
     def hgather(k):
-        act(R("H%d" % (k % 2)), IX(R("ST"), R("W16", k * CW, k * CW + CW)), AF.Copy)
+        act(R("H%d" % (k % NBF)), IX(R("ST"), R("W16", k * CW, k * CW + CW)), AF.Copy)
 
     def diff(k):
-        tt(R("D%d" % (k % 2)), IX(R("XS"), R("W16", k * CW, k * CW + CW)), R("B%d" % k), OP.subtract)
+        tt(R("D%d" % (k % NBF)), IX(R("XS"), R("W16", k * CW, k * CW + CW)), R("B%d" % k), OP.subtract)
 
-    def dsum1(k): wrapmm(dbank(k), "ZM", "D%d" % (k % 2), True, False)
+    def dsum1(k): wrapmm(dbank(k), "ZM", "D%d" % (k % NBF), True, False)
 
     def dsum2(k):
-        ts(R("R%d" % (k % 2)), R("D%d" % (k % 2)), 0.0, OP.max)
-        wrapmm(dbank(k), "Z2", "R%d" % (k % 2), False, False)
+        ts(R("R%d" % (k % NBF)), R("D%d" % (k % NBF)), 0.0, OP.max)
+        wrapmm(dbank(k), "Z2", "R%d" % (k % NBF), False, False)
 
     def other(k):
         a, b = k * CW, k * CW + CW
-        wrapmm(hbank(k, 0), "ZY", "H%d" % (k % 2), True, True)
-        tt(R("O0", a, b), hbank(k, 0), R("KF", a, b), OP.not_equal)
+        wrapmm(hbank(k), "ZY", "H%d" % (k % NBF), True, True)
+        tt(R("O0", a, b), hbank(k), R("KF", a, b), OP.not_equal)
         mm(dbank(k), R("I8N"), R("DA", a, b), False, False)
         mm(dbank(k), R("I8"), R("O0", a, b), False, True)
 
@@ -446,37 +533,44 @@ def rank_program(g, core, T, topo):
 
     def verdict2(k):
         a, b = k * CW, k * CW + CW
-        hx = hbank(k, 1)
-        for o, (m32, mn, m1) in ((R("VA_", a, b), ("G32", "GN", "GG")), (R("VB_", a, b), ("RS32", "RSN", "RS")), (hx, ("RS32", "RSN", "RS"))):
+        hx = nbank(k, 1)
+        for o, (m32, mn, m1) in ((R("VA_", a, b), ("G32", "GN", "GG")), (nbank(k, 0), ("RS32", "RSN", "RS")), (hx, ("RS32", "RSN", "RS"))):
             mm(o, R(mn), R("O0", a, b), True, False)
             mm(o, R(m1), R("DA", a, b), False, False)
             mm(o, R(m32), R("FF", a, b), False, o is not hx)
         mm(hx, R("GR"), R("GB", a, b), False, False)
         mm(hx, R("YRN"), R("YG", a, b), False, True)
-        mm(hbank(k, 2), R("YR"), R("YG", a, b), True, True)
+        mm(nbank(k, 2), R("YR"), R("YG", a, b), True, True)
 
     def outcome(k):
         a, b = k * CW, k * CW + CW
         ts(R("PM", a, b), R("VA_", a, b), 0.0, OP.is_lt)
         scan(R("PP", a, b), R("PM", a, b), R("PM", a, b), R("PP", a - 1, a) if k else 0.0, OP.add, OP.max)
-        ts(R("MU", a, b), R("VB_", a, b), co(14), OP.is_gt)
-        tt(R("T2", a, b), hbank(k, 1), R("MU", a, b), OP.mult)
-        tt(R("QQ", a, b), hbank(k, 2), R("T2", a, b), OP.add)
+        ts(R("MU", a, b), nbank(k, 0), co(14), OP.is_gt)
+        tt(R("T2", a, b), nbank(k, 1), R("MU", a, b), OP.mult)
+        tt(R("QQ", a, b), nbank(k, 2), R("T2", a, b), OP.add)
         ts(R("DD", a, b), R("QQ", a, b), 10, OP.arith_shift_right, 31, OP.bitwise_and)
 
-    def count_lists():
+    def proposals_part(j):
+        a, b = PARTS[j], PARTS[j + 1]
         for k in range(2):
-            act(R("JK"), R("PP"), AF.Sign, bias=R("RB", k, k + 1), scale=-1.0, acc=R("AC", k, k + 1))
-        act(R("NG"), R("VA_"), AF.Sign, bias=-0.5, acc=R("AC", 6, 7))
-        act(R("MN"), R("VA_"), AF.Sign, bias=-100.0)
+            act(R("JK", 512 * k + a, 512 * k + b), R("PP", a, b), AF.Sign, bias=R("RB", k, k + 1), scale=-1.0, acc=R("AC", 8 * j + k, 8 * j + k + 1))
 
-    def repair_scan():
-        scan(R("RP"), R("NG"), R("MN"), 0.0, OP.add, OP.subtract)
+    def repairs_part(j):
+        a, b = PARTS[j], PARTS[j + 1]
+        act(R("NG", a, b), R("VA_", a, b), AF.Sign, bias=-0.5, acc=R("AC", 8 * j + 6, 8 * j + 7))
+        act(R("MN", a, b), R("VA_", a, b), AF.Sign, bias=-100.0)
+        scan(R("RP", a, b), R("NG", a, b), R("MN", a, b), R("RP", a - 1, a) if j else 0.0, OP.add, OP.subtract)
         for k in range(4):
-            act(R("JK"), R("RP"), AF.Sign, bias=R("RB", k, k + 1), scale=-0.5, acc=R("AC", 2 + k, 3 + k))
+            act(R("JK", 512 * k + 1024 + a, 512 * k + 1024 + b), R("RP", a, b), AF.Sign, bias=R("RB", k, k + 1), scale=-0.5, acc=R("AC", 8 * j + 2 + k, 8 * j + 3 + k))
+
+    def lanes_part(j):
+        a, b = PARTS[j], PARTS[j + 1]
+        scatter(R("ST"), R("A16", a // 16, b // 16), R("DD", a, b))
 
     def retypes():
-        ts(R("PL16"), R("AC", 0, 2), 0.5, OP.mult, 256.0, OP.add)
+        tt(R("AC", 16, 18), R("AC", 0, 2), R("AC", 8, 10), OP.add)
+        ts(R("PL16"), R("AC", 16, 18), 0.5, OP.mult, 256.0, OP.add)
         cp(R("OG"), IX(R("O0"), R("PL16")))
         cp(R("KG"), IX(R("KF"), R("PL16")))
         cp(R("WG"), IX(R("WF"), R("PL16")))
@@ -503,10 +597,11 @@ def rank_program(g, core, T, topo):
         scatter(R("ST"), R("OX16"), R("KD"))
 
     def count_good():
-        ts(R("GC1"), R("AC", 6, 7), -0.5, OP.mult, 256.0, OP.add)
+        tt(R("AC", 22, 23), R("AC", 6, 7), R("AC", 14, 15), OP.add)
+        ts(R("GC1"), R("AC", 22, 23), -0.5, OP.mult, 256.0, OP.add)
         tt(R("GS"), R("GC1"), R("GP"), OP.subtract)
-        mm(R("LB", 0, 1), R("SF"), R("GS"), True, True)
-        cp(R("BI1"), R("LB", 0, 1))
+        mm(R(GBK, 0, 1), R("SF"), R("GS"), True, True)
+        cp(R("BI1"), R(GBK, 0, 1))
         ts(R("BJ"), R("BI1"), 255, OP.bitwise_and)
         tt(R("LM"), R("LB0"), R("BJ"), OP.add)
 
@@ -515,7 +610,7 @@ def rank_program(g, core, T, topo):
         mask = sum(1 << e for e in eng)
         rid, pid, _ = topo.addr(dst)
         x, y = R(buf), R(land)
-        emit("G", lambda: g.remote_dma(y[0], x[0], T.sem[sem], T.sem.loc, pid, rid, mask), x[1], [], count=len(eng))
+        sent[sem] = emit("G", lambda: g.remote_dma(y[0], x[0], T.sem[sem], T.sem.loc, pid, rid, mask), x[1], [], 1.0, count=len(eng))
         extra["loc"] = extra.get("loc", 0) + len(eng)
 
     def helper(t): return T.cores[(rank + 1 + t % (n_ranks - 1)) % n_ranks]
@@ -523,7 +618,8 @@ def rank_program(g, core, T, topo):
 
     def request(t):
         c = (ST0 * t) % V
-        ts(R("RN1"), R("AC", 2, 6), 0.5, OP.mult, 256.0, OP.add)
+        tt(R("AC", 18, 22), R("AC", 2, 6), R("AC", 10, 14), OP.add)
+        ts(R("RN1"), R("AC", 18, 22), 0.5, OP.mult, 256.0, OP.add)
         ts(R("RM"), R("RN1"), float(LN), OP.is_ge)
         tt(R("RK"), R("RM"), R("RC"), OP.mult)
         tt(R("RL"), R("RN1"), R("RK"), OP.add)
@@ -545,10 +641,10 @@ def rank_program(g, core, T, topo):
     def service0(t):
         X = "QX%d" % t
         landed(X, "rq%d" % t, len(topo.engines(asker(t), core)[:8]))
-        wrapmm(R("HA_", 0, 4), "ZU", X, True, True)
+        wrapmm(R(UB, 0, 4), "ZU", X, True, True)
 
     def service1(t):
-        cp(R("UI1"), R("HA_", 0, 4))
+        cp(R("UI1"), R(UB, 0, 4))
         ts(R("UA"), R("UI1"), V - 1, OP.bitwise_and)
         tt(R("UU"), R("UA"), R("UA"), OP.mult)
         ts(R("TM"), R("UA"), 2.0, OP.mult, 1.0, OP.add)
@@ -566,12 +662,12 @@ def rank_program(g, core, T, topo):
             tt(R("DX", 64 * m, 64 * m + 64), IX(R("XS"), R("C16", 4 * m, 4 * m + 4)), R(X), OP.subtract)
         if b == 16:
             ts(R("RX2"), R("DX"), 0.0, OP.max)
-            wrapmm(R("LB", 0, 64), "ZV", "VG", True, False)
-            wrapmm(R("LB", 0, 64), "ZM16", "DX", False, False)
-            wrapmm(R("LB", 0, 64), "Z32", "RX2", False, True)
+            wrapmm(R(KB, 0, 64), "ZV", "VG", True, False)
+            wrapmm(R(KB, 0, 64), "ZM16", "DX", False, False)
+            wrapmm(R(KB, 0, 64), "Z32", "RX2", False, True)
 
     def service3(t):
-        tt(R("KEY"), R("LB", 0, 64), R("M64"), OP.add)
+        tt(R("KEY"), R(KB, 0, 64), R("M64"), OP.add)
         for k in range(4): red(R("KM1", k, k + 1), R("KEY", k, 64, 4), OP.min)
         cp(R("MI"), R("KM1"))
         ts(R("NN"), R("KM1"), 0.0, OP.is_ge, 4096.0, OP.mult)
@@ -594,7 +690,7 @@ def rank_program(g, core, T, topo):
         tt(R("FM"), R("MK"), R("FLG"), OP.mult)
         tt(R("DM"), R("DW"), R("FM"), OP.mult)
         win, off, x, y = R("WD"), R("RA16"), R("WO1"), R("DM")
-        emit("V", lambda: g.vector.tensor_tensor(win[0].indirect(off[0]), x[0], y[0], OP.add), x[1] + y[1] + off[1], win[1])
+        emit("V", lambda: g.vector.tensor_tensor(win[0].indirect(off[0]), x[0], y[0], OP.add), x[1] + y[1] + off[1], win[1], 0.05 + SL * SCA * CY)
 
     for t in range(RO):
         if t == 0: consts2()
@@ -630,13 +726,15 @@ def rank_program(g, core, T, topo):
             if k: verdict1(k - 1)
             if k < NCH: dsum2(k)
             if k: verdict2(k - 1)
+            if k > 1 and k - 1 == PARTS[1] // CW:
+                proposals_part(0)
+                repairs_part(0)
         outcome(NCH - 1)
-        count_lists()
-        if t == RO - 1:
-            repair_scan()
-            request(t)
-        scatter(R("ST"), R("A16"), R("DD"))
-        if t < RO - 1: repair_scan()
+        lanes_part(0)
+        proposals_part(1)
+        repairs_part(1)
+        if t == RO - 1: request(t)
+        lanes_part(1)
         retypes()
     service0(RO - 1)
     service1(RO - 1)
@@ -649,6 +747,7 @@ def rank_program(g, core, T, topo):
     dma("G", HBM(T.yv[:, :]), R("ST", 0, V, ps=slice(2, 128, 16)))
     merge(RO - 1)
     dma("Y", HBM(T.ym[:, :]), R("WD", 0, V))
+    schedule()
     for q in ("V", "S", "T", "G"):
         g.wait_ge(T.sem["s" + q], cnt[q])
     for k in range(ndma[0]): g.wait_ge(T.sem["dm%d" % k], 16)

@@ -14,7 +14,9 @@ NBF = 4
 TF = (2, 4)
 SB = 4
 PARTS = (0, 384, 512)
-CY, GAT, SCA, PEC, WK, LOOK = 0.83e-3, 1.5, 3.0, 0.5e-3, 0.1, 0.0
+CY, GAT, SCA, PEC, WK, LOOK = 0.83e-3, 1.8, 4.0, 0.55e-3, 0.13, 0.1
+AS = ()
+MADE, PASSES, NOISE = {}, 260, 2.5
 KB, GBK, UB, NBK = "DA_", "DB_", "HA_", ("LA", "LB", "VB_")
 
 BFB, F32, I32, U16 = "bfloat16", "float32", "int32", "uint16"
@@ -35,16 +37,16 @@ for _n, _c, _d in [
     ("JR", 512, F32), ("BR", NB, BFB), ("ER", NB, BFB), ("ZR", NB, F32), ("DG", 64, F32), ("TR", 64, F32), ("RB", 4, F32), ("RC", 4, F32), ("RE", 2, F32),
     ("M16", 16, F32), ("M64", 64, F32), ("YI", 64 * 7, I32), ("YD", 128, BFB), ("GTB", 1040, BFB), ("YHM", 8, BFB),
     ("PIN", NB, BFB), ("BPI", NB, F32), ("BPX", NB, F32), ("PW", NB, F32), ("EM", NB, BFB), ("EMC", NB, BFB), ("OFF", 10, F32), ("OF16", 10, U16),
-    ("FR", 512, BFB), ("FL16", 32, U16), ("AJ", 96, BFB), ("E", 512, BFB), ("A16", 32, U16),
+    ("FR", 512, BFB), ("FL16", 32, U16), ("AJ", 96, BFB), ("E", 512, BFB), ("AR", 1024, BFB), ("A16", 32, U16),
     ("XR0", 576, F32), ("YG", 512, BFB), ("Y16", 32, U16), ("GB", 512, BFB),
-    ("KF", 576, F32), ("K16", 512, U16), ("DA", 512, BFB), ("WF", 576, F32), ("W16", 512, U16), ("LIM", 2, F32),
+    ("KF", 576, F32), ("K16", 512, U16), ("DA", 576, BFB), ("WF", 576, F32), ("W16", 512, U16), ("LIM", 2, F32),
     ("O0", 576, BFB), ("FF", 576, BFB), ("PM", 512, BFB), ("PP", 512, BFB), ("MU", 512, BFB), ("T2", 512, F32), ("QQ", 512, I32), ("DD", 512, I32),
-    ("NG", 512, BFB), ("MN", 512, BFB), ("RP", 512, BFB), ("JK", 3072, BFB), ("AC", 24, F32),
+    ("NG", 576, BFB), ("MN", 576, BFB), ("RP", 576, BFB), ("JK", 3456, BFB), ("AC", 24, F32),
     ("PL16", 2, U16), ("WKG", 160, F32), ("OKR", 96, BFB), ("FI", 32, F32),
     ("WW", 10, F32), ("EQ", 128, F32), ("OX16", 2, U16), ("KI", 64, I32), ("GC", 3, F32), ("BI", 2, I32),
-    ("RN", 20, F32), ("RL16", 4, U16), ("XG", 128, F32), ("X4", 16, F32), ("RA16", 4, U16),
+    ("RX", 4, F32), ("RL16", 4, U16), ("XG", 128, F32), ("RA16", 4, U16),
     ("UI", 32, I32), ("BS", 8, F32), ("CI", 128, I32), ("C16", 64, U16), ("DX", 1024, BFB), ("RX2", 1024, BFB), ("VG", 1024, BFB),
-    ("KEY", 64, F32), ("KM", 16, F32), ("BB16", 4, U16), ("FLG", 64, BFB), ("WO", 320, F32), ("YO", V, F32),
+    ("KEY", 64, F32), ("KMI", 4, I32), ("NN", 4, F32), ("BB16", 4, U16), ("FLG", 64, BFB), ("WO", 320, F32), ("YO", V, F32),
 ]:
     _buf(_n, _c, _d)
 _CHK = ["B%d" % k for k in range(NCH)] + [c + "%d" % k for c in "HDR" for k in range(NBF)]
@@ -57,18 +59,17 @@ for _t in range(RO):
 PART = {}
 for _k, _n in enumerate(("Z", "ZM", "Z2", "Z32", "ZM16", "ZY", "ZU", "ZV", "Z0")): PART[_n] = ("ZZ", 144 * _k, 144)
 _buf("Z016", 144, BFB)
-for _k, _n in enumerate(("LT", "GR2", "G016", "G32", "GN", "RS", "RS32", "RSN", "YR", "YRN", "GR", "I8", "I8N", "US", "PL", "GR3")): PART[_n] = ("MX", 128 * _k, 128)
+for _k, _n in enumerate(("LT", "GR2", "G016", "G32", "GN", "RS", "RS32", "RSN", "YR", "YRN", "GR", "I8", "I8N", "US", "PL", "GR3", "PLN")): PART[_n] = ("MX", 128 * _k, 128)
 for _n, _b, _w, _l in (("HXA", "HX", 128, 0), ("HXB", "HX", 128, 1), ("A1", "AJ", 32, 1), ("A2", "AJ", 32, 2), ("AJ0", "AJ", 32, 0),
                        ("WG", "WKG", 32, 0), ("KG", "WKG", 32, 1), ("WK", "WKG", 32, 2), ("KK", "WKG", 32, 3), ("WDG", "WKG", 32, 4),
                        ("OG", "OKR", 32, 0), ("KL", "OKR", 32, 1), ("OR", "OKR", 32, 2), ("EQ1", "EQ", 64, 0), ("EQ2", "EQ", 64, 1),
                        ("W2", "WW", 2, 0), ("DU", "WW", 2, 1), ("DE", "WW", 2, 2), ("DE2", "WW", 2, 3), ("OX", "WW", 2, 4),
                        ("KI1", "KI", 32, 0), ("KD", "KI", 32, 1), ("LM", "LIM", 1, 0), ("LB0", "LIM", 1, 1),
                        ("GC1", "GC", 1, 0), ("GP", "GC", 1, 1), ("GS", "GC", 1, 2), ("BI1", "BI", 1, 0), ("BJ", "BI", 1, 1),
-                       ("RN1", "RN", 4, 0), ("RM", "RN", 4, 1), ("RK", "RN", 4, 2), ("RL", "RN", 4, 3), ("RX", "RN", 4, 4),
-                       ("XG1", "XG", 64, 0), ("XD", "XG", 64, 1), ("X1", "X4", 4, 0), ("X2", "X4", 4, 1), ("X3", "X4", 4, 2), ("X5", "X4", 4, 3),
+                       ("XG1", "XG", 64, 0), ("XD", "XG", 64, 1),
                        ("UI1", "UI", 4, 0), ("UA", "UI", 4, 1), ("UU", "UI", 4, 2), ("UV", "UI", 4, 3), ("MI", "UI", 4, 4), ("MJ", "UI", 4, 5), ("P2", "UI", 4, 6), ("P3", "UI", 4, 7),
                        ("BS1", "BS", 4, 0), ("TM", "BS", 4, 1), ("CI1", "CI", 64, 0), ("CA", "CI", 64, 1),
-                       ("KM1", "KM", 4, 0), ("P1", "KM", 4, 1), ("NN", "KM", 4, 2), ("P4", "KM", 4, 3),
+                       ("KM1", "KMI", 4, 0),
                        ("WO1", "WO", 64, 0), ("MK", "WO", 64, 1), ("FM", "WO", 64, 2), ("DW", "WO", 64, 3), ("DM", "WO", 64, 4),
                        ("YI0", "YI", 64, 0), ("YJ", "YI", 64, 1), ("Y2", "YI", 64, 2), ("Y3", "YI", 64, 3), ("Y4", "YI", 64, 4), ("Y5", "YI", 64, 5), ("Y6", "YI", 64, 6)):
     PART[_n] = (_b, _w * _l, _w)
@@ -162,32 +163,54 @@ def rank_program(g, core, T, topo):
                         h.append((i, w, r))
             npred[i] = len(pred)
             for j, wait in pred.items(): succ[j].append((i, wait))
+        prec = [[] for _ in range(n)]
+        for i in range(n):
+            for k, (j, w) in enumerate(succ[i]):
+                d = nodes[i][5] + WK if w else 0.0
+                succ[i][k] = (j, d)
+                prec[j].append((i, d))
         far = [0.0] * n
         for i in range(n - 1, -1, -1):
-            far[i] = nodes[i][4] + nodes[i][5] + max([far[j] + (WK if w else 0.0) for j, w in succ[i]] or [0.0])
-        ready, free, order, left = {}, {}, [], n
-        at = [0.0] * n
-        for i in range(n):
-            if npred[i] == 0: ready.setdefault(nodes[i][0], []).append(i)
-        while left:
-            best = None
-            for q, l in ready.items():
-                if not l: continue
-                f = free.get(q, 0.0)
-                t0 = max(f, min(at[i] for i in l))
-                i = max((i for i in l if at[i] <= t0 + LOOK), key=lambda i: (far[i] - max(0.0, at[i] - t0), -i))
-                t1 = max(f, at[i])
-                if best is None or t1 < best[0]: best = (t1, i, q)
-            t1, i, q = best
-            ready[q].remove(i)
-            order.append((t1, i))
-            left -= 1
-            if q != "N": free[q] = t1 + nodes[i][4]
-            for j, w in succ[i]:
-                at[j] = max(at[j], t1 + nodes[i][4] + (nodes[i][5] + WK if w else 0.0))
-                npred[j] -= 1
-                if npred[j] == 0: ready.setdefault(nodes[j][0], []).append(j)
-        for _, i in order:
+            far[i] = nodes[i][4] + max([far[j] + d for j, d in succ[i]] or [nodes[i][5]])
+
+        def listed(edges, back, prio):
+            left, at, end, order = [len(x) for x in back], [0.0] * n, [0.0] * n, []
+            ready, free = {}, {}
+            for i in range(n):
+                if left[i] == 0: ready.setdefault(nodes[i][0], []).append(i)
+            for _ in range(n):
+                best = None
+                for q, l in ready.items():
+                    if not l: continue
+                    t0 = max(free.get(q, 0.0), min([at[i] for i in l]))
+                    if best is None or t0 < best[0]: best = (t0, q)
+                t0, q = best
+                l = ready[q]
+                i = max([i for i in l if at[i] <= t0 + LOOK], key=lambda i: prio[i])
+                l.remove(i)
+                t1 = max(t0, at[i])
+                order.append((t1, i))
+                end[i] = t1 + nodes[i][4]
+                if q != "N": free[q] = end[i]
+                for j, d in edges[i]:
+                    at[j] = max(at[j], end[i] + d)
+                    left[j] -= 1
+                    if left[j] == 0: ready.setdefault(nodes[j][0], []).append(j)
+            return order, end
+
+        if "order" not in MADE:
+            prio, best, seed = far, None, 1
+            for k in range(PASSES):
+                order, end = listed(succ, prec, prio)
+                if best is None or max(end) < best[0]: best = (max(end), order, prio)
+                prio = listed(prec, succ, end)[1]
+                if k % 4 == 3:
+                    prio = []
+                    for i in range(n):
+                        seed = seed * 1103515245 + 12345 & 0x7fffffff
+                        prio.append(best[2][i] + NOISE * ((seed >> 8) % 1000) / 1000.0)
+            MADE["order"] = best[1]
+        for _, i in MADE["order"]:
             q, calls = nodes[i][0], nodes[i][1]
             for fn, rd, wr, dma, count in calls:
                 if q == "N": fn()
@@ -423,7 +446,7 @@ def rank_program(g, core, T, topo):
             ts(R("DG", 16 * k, 16 * k + 16), R("CMI", 0, 16), R("PC"), OP.is_equal)
             ts(R("RB", k, k + 1), R("PC"), 16.0 * k + 0.5, OP.add)
             ts(R("RC", k, k + 1), R("PC"), 16.0 * k, OP.add)
-        for n in ("WF", "KF", "O0", "FF"): fill(R(n, LN, 576), 0.0)
+        for n in ("WF", "KF", "O0", "FF", "DA"): fill(R(n, LN, 576), 0.0)
         ts(R("LB0"), R("TH"), 8192.0, OP.add)
         cp(R("LM"), R("LB0"))
 
@@ -443,11 +466,14 @@ def rank_program(g, core, T, topo):
         sc(R("SF"), R("ON"), ri(0))
         sc(R("PL"), R("US"), 2.0)
         tt(R("PL"), R("PL"), R("ID"), OP.subtract)
+        sc(R("PLN"), R("PL"), -1.0)
+        fill(R("NG", LN, 576), 1.0)
+        fill(R("MN", LN, 576), -1.0)
         role(11, [(0, 32), (1, 1)])
         ts(R("YHM"), R("GM"), co(11), OP.mult)
-        ts(R("RE", 0, 1), R("PC"), 1.0 - 10000.0, OP.add)
-        ts(R("RE", 1, 2), R("PC"), 17.0 - 10000.0, OP.add)
-        for k in range(2): ts(R("TR", 32 * k, 32 * k + 32), R("JR", 0, 32), R("RC", k, k + 1), OP.is_lt)
+        ts(R("RE", 0, 1), R("PC"), DUMP + 1.0 - 10000.0, OP.add)
+        ts(R("RE", 1, 2), R("PC"), DUMP + 17.0 - 10000.0, OP.add)
+        for k in range(2): ts(R("TR", 32 * k, 32 * k + 32), R("JR", 0, 32), R("RC", k, k + 1), OP.is_lt, 10000.0, OP.mult)
 
     def lanes(t):
         c = (ST0 * t) % V
@@ -483,9 +509,13 @@ def rank_program(g, core, T, topo):
         cp(R("YG"), IX(R("ST"), R("A16")))
         wrapmm(R("LB", 0, 32), "ZY", "YG", True, True)
         mm(R("VA_"), R("G016"), R("FR"), True, False)
+        if c:
+            ts(R("AR", 0, 512), R("FR"), float(128 - b0), OP.is_ge, -2048.0, OP.mult)
+            ts(R("AR", 512, 1024), R("FR"), 128.0, OP.is_ge, float(2048 - c), OP.mult)
+            for k in range(2): mm(R("VA_"), R("ID"), R("AR", 512 * k, 512 * k + 512), False, False)
         mm(R("VA_"), R("GG"), R("E"), False, True)
         if t: service1(t - 1)
-        act(R("XR0", 0, LN), R("VA_"), AF.Copy)
+        act(R("XR0", 0, LN), R("VA_"), AF.Identity, bias=float(c))
         fill(R("FB", 0, LN), 0.0)
 
     def types(k):
@@ -515,11 +545,13 @@ def rank_program(g, core, T, topo):
     def diff(k):
         tt(R("D%d" % (k % NBF)), IX(R("XS"), R("W16", k * CW, k * CW + CW)), R("B%d" % k), OP.subtract)
 
-    def dsum1(k): wrapmm(dbank(k), "ZM", "D%d" % (k % NBF), True, False)
+    def dsum1(k):
+        if k in AS: act(R("R%d" % (k % NBF)), R("D%d" % (k % NBF)), AF.Abs)
+        else: wrapmm(dbank(k), "ZM", "D%d" % (k % NBF), True, False)
 
     def dsum2(k):
-        ts(R("R%d" % (k % NBF)), R("D%d" % (k % NBF)), 0.0, OP.max)
-        wrapmm(dbank(k), "Z2", "R%d" % (k % NBF), False, False)
+        if k not in AS: ts(R("R%d" % (k % NBF)), R("D%d" % (k % NBF)), 0.0, OP.max)
+        wrapmm(dbank(k), "Z" if k in AS else "Z2", "R%d" % (k % NBF), k in AS, False)
 
     def other(k):
         a, b = k * CW, k * CW + CW
@@ -554,15 +586,16 @@ def rank_program(g, core, T, topo):
     def proposals_part(j):
         a, b = PARTS[j], PARTS[j + 1]
         for k in range(2):
-            act(R("JK", 512 * k + a, 512 * k + b), R("PP", a, b), AF.Sign, bias=R("RB", k, k + 1), scale=-1.0, acc=R("AC", 8 * j + k, 8 * j + k + 1))
+            act(R("JK", 576 * k + a, 576 * k + b), R("PP", a, b), AF.Sign, bias=R("RB", k, k + 1), scale=-1.0, acc=R("AC", 8 * j + k, 8 * j + k + 1))
 
     def repairs_part(j):
         a, b = PARTS[j], PARTS[j + 1]
         act(R("NG", a, b), R("VA_", a, b), AF.Sign, bias=-0.5, acc=R("AC", 8 * j + 6, 8 * j + 7))
         act(R("MN", a, b), R("VA_", a, b), AF.Sign, bias=-100.0)
+        if j: b += SL
         scan(R("RP", a, b), R("NG", a, b), R("MN", a, b), R("RP", a - 1, a) if j else 0.0, OP.add, OP.subtract)
         for k in range(4):
-            act(R("JK", 512 * k + 1024 + a, 512 * k + 1024 + b), R("RP", a, b), AF.Sign, bias=R("RB", k, k + 1), scale=-0.5, acc=R("AC", 8 * j + 2 + k, 8 * j + 3 + k))
+            act(R("JK", 576 * k + 1152 + a, 576 * k + 1152 + b), R("RP", a, b), AF.Sign, bias=R("RB", k, k + 1), scale=-0.5, acc=R("AC", 8 * j + 2 + k, 8 * j + 3 + k))
 
     def lanes_part(j):
         a, b = PARTS[j], PARTS[j + 1]
@@ -574,9 +607,9 @@ def rank_program(g, core, T, topo):
         cp(R("OG"), IX(R("O0"), R("PL16")))
         cp(R("KG"), IX(R("KF"), R("PL16")))
         cp(R("WG"), IX(R("WF"), R("PL16")))
-        ts(R("KL"), R("KG"), float(TY), OP.is_lt)
-        tt(R("OR"), R("OG"), R("KL"), OP.mult)
-        mm(R("LA", 0, 32), R("PL"), R("OR"), True, True)
+        cp(R("KL"), IX(R("DA"), R("PL16")))
+        mm(R("LA", 0, 32), R("PL"), R("OG"), True, False)
+        mm(R("LA", 0, 32), R("PLN"), R("KL"), False, True)
         ts(R("WG"), R("WG"), float(-DUMP), OP.add)
         ts(R("FI"), R("LA", 0, 32), 0.0, OP.is_lt)
         tt(R("WK"), R("WG"), R("FI"), OP.mult)
@@ -590,10 +623,8 @@ def rank_program(g, core, T, topo):
         cp(R("KI1"), R("LB", 0, 32))
         for k in range(2): red(R("DU", k, k + 1), R("EQ2", 32 * k, 32 * k + 32), OP.max)
         ts(R("KD"), R("KI1"), 10, OP.arith_shift_right, 31, OP.bitwise_and)
-        ts(R("DE"), R("DU"), 10000.0, OP.mult)
-        tt(R("DE2"), R("DE"), R("RE"), OP.add)
-        tt(R("OX"), R("W2"), R("DE2"), OP.max)
-        ts(R("OX16"), R("OX"), float(DUMP), OP.add)
+        ts(R("DE"), R("W2"), float(DUMP), OP.add)
+        for k in range(2): ts(R("OX16", k, k + 1), R("DU", k, k + 1), R("RE", k, k + 1), OP.add, R("DE", k, k + 1), OP.max)
         scatter(R("ST"), R("OX16"), R("KD"))
 
     def count_good():
@@ -617,24 +648,12 @@ def rank_program(g, core, T, topo):
     def asker(t): return T.cores[(rank - 1 - t % (n_ranks - 1)) % n_ranks]
 
     def request(t):
-        c = (ST0 * t) % V
         tt(R("AC", 18, 22), R("AC", 2, 6), R("AC", 10, 14), OP.add)
-        ts(R("RN1"), R("AC", 18, 22), 0.5, OP.mult, 256.0, OP.add)
-        ts(R("RM"), R("RN1"), float(LN), OP.is_ge)
-        tt(R("RK"), R("RM"), R("RC"), OP.mult)
-        tt(R("RL"), R("RN1"), R("RK"), OP.add)
-        cp(R("RL16"), R("RL"))
+        ts(R("RL16"), R("AC", 18, 22), 0.5, OP.mult, 288.0, OP.add)
         cp(R("XG1"), IX(R("XR0"), R("RL16")))
         tt(R("XD"), R("XG1"), R("DG"), OP.mult)
         for k in range(4): red(R("RX", k, k + 1), R("XD", 16 * k, 16 * k + 16), OP.add)
-        if c:
-            ts(R("X1"), R("RX"), float(2048 - c), OP.is_ge, -2048.0, OP.mult)
-            ts(R("X2"), R("RX"), 2048.0, OP.is_ge, float(2048 - c), OP.mult)
-            tt(R("X3"), R("RX"), R("X1"), OP.add)
-            tt(R("X5"), R("X3"), R("X2"), OP.add)
-            ts(R("RA16"), R("X5"), float(c), OP.add)
-        else:
-            cp(R("RA16"), R("RX"))
+        cp(R("RA16"), R("RX"))
         cp(R("XQ%d" % t), IX(R("XS"), R("RA16")))
         send("XQ%d" % t, "QX%d" % t, helper(t), "rq%d" % t)
 
@@ -669,14 +688,11 @@ def rank_program(g, core, T, topo):
     def service3(t):
         tt(R("KEY"), R(KB, 0, 64), R("M64"), OP.add)
         for k in range(4): red(R("KM1", k, k + 1), R("KEY", k, 64, 4), OP.min)
-        cp(R("MI"), R("KM1"))
         ts(R("NN"), R("KM1"), 0.0, OP.is_ge, 4096.0, OP.mult)
-        ts(R("MJ"), R("MI"), 15, OP.bitwise_and)
-        tt(R("P1"), R("MJ"), R("TM"), OP.mult)
-        tt(R("P2"), R("P1"), R("BS1"), OP.add)
+        ts(R("MJ"), R("KM1"), 15, OP.bitwise_and)
+        for k in range(4): ts(R("P2", k, k + 1), R("MJ", k, k + 1), R("TM", k, k + 1), OP.mult, R("BS1", k, k + 1), OP.add)
         ts(R("P3"), R("P2"), V - 1, OP.bitwise_and)
-        tt(R("P4"), R("P3"), R("NN"), OP.add)
-        ts(R("BB16"), R("P4"), float(MARK), OP.min)
+        for k in range(4): ts(R("BB16", k, k + 1), R("P3", k, k + 1), R("NN", k, k + 1), OP.add, float(MARK), OP.min)
         cp(R("WR%d" % t), IX(R("WD"), R("BB16")))
         send("WR%d" % t, "QW%d" % t, asker(t), "rp%d" % t)
 
@@ -706,7 +722,7 @@ def rank_program(g, core, T, topo):
         else:
             service3(t - 1)
         for k in range(TF[1], NCH): types(k)
-        ts(R("DA"), R("K16"), float(TY), OP.is_equal)
+        ts(R("DA", 0, LN), R("K16"), float(TY), OP.is_equal)
         dma("Y", R("SVB", 0, V, ps=slice(2, 128, 16)), R("ST", 0, V, ps=slice(2, 128, 16)))
         if t: count_good()
         ts(R("GP"), R("BPI", 127, 128), -1.0, OP.mult, float(LN), OP.add)

from concourse.mybir import AluOpType as OP, AxisListType, ActivationFunctionType as AF

V, TY, LN, SL, RT, RO, ST0 = 2048, 1024, 512, 64, 32, 4, 640
NB = 160
FBW = 8704
STW = 2736
DUMP = 2688
MARK = 2736
WDW = 2752
XSW = 2640
NCH = 8
CW = LN // NCH
NBF = 4
TF = (2, 4)
SB = 4
PARTS = (0, 384, 512)
CY, GAT, SCA, PEC, WK, LOOK = 0.83e-3, 1.8, 4.0, 0.55e-3, 0.13, 0.1
AS = ()
MADE, PASSES, NOISE = {}, 260, 2.5
KB, GBK, UB, NBK = "DA_", "DB_", "HA_", ("LA", "LB", "VB_")

BFB, F32, I32, U16 = "bfloat16", "float32", "int32", "uint16"
SCRATCH = {}


def _buf(name, cols, d, where="sbuf"):
    SCRATCH[name] = (where, [128, cols], d)


for _n, _c, _d in [
    ("WI", V, I32), ("WD", WDW, F32), ("XS", XSW, BFB), ("RQ", 1040, I32), ("SG", 1040, BFB),
    ("HS", 128, I32), ("VS", 128, I32), ("TH", 1, I32), ("HX", 256, I32),
    ("HB3", 384, BFB), ("ST", STW, BFB), ("SVB", V, BFB), ("FB", FBW, BFB),
    ("GM", 8, BFB), ("GG", 128, BFB), ("ID", 128, BFB), ("ON", 128, BFB), ("ZZ", 144 * 9, BFB), ("WV", 2048, BFB), ("PWM", 2048, BFB),
    ("MX", 128 * 17, BFB), ("GF", 128, F32), ("RF", 128, F32), ("SF", 128, F32),
    ("PI", 1, I32), ("PA", 1, I32), ("PC", 1, F32), ("PC1", 1, F32), ("CO", 32, F32), ("RI", 16, F32), ("CMI", 128, BFB), ("CMJ", 128, BFB), ("GK", 128, BFB),
    ("JR", 512, F32), ("BR", NB, BFB), ("ER", NB, BFB), ("ZR", NB, F32), ("DG", 64, F32), ("TR", 64, F32), ("RB", 4, F32), ("RC", 4, F32), ("RE", 2, F32),
    ("M16", 16, F32), ("M64", 64, F32), ("YI", 64 * 7, I32), ("YD", 128, BFB), ("GTB", 1040, BFB), ("YHM", 8, BFB),
    ("PIN", NB, BFB), ("BPI", NB, F32), ("BPX", NB, F32), ("PW", NB, F32), ("EM", NB, BFB), ("EMC", NB, BFB), ("OFF", 10, F32), ("OF16", 10, U16),
    ("FR", 512, BFB), ("FL16", 32, U16), ("AJ", 96, BFB), ("E", 512, BFB), ("AR", 1024, BFB), ("A16", 32, U16),
    ("XR0", 576, F32), ("YG", 512, BFB), ("Y16", 32, U16), ("GB", 512, BFB),
    ("KF", 576, F32), ("K16", 512, U16), ("DA", 576, BFB), ("WF", 576, F32), ("W16", 512, U16), ("LIM", 2, F32),
    ("O0", 576, BFB), ("FF", 576, BFB), ("PM", 512, BFB), ("PP", 512, BFB), ("MU", 512, BFB), ("T2", 512, F32), ("QQ", 512, I32), ("DD", 512, I32),
    ("NG", 576, BFB), ("MN", 576, BFB), ("RP", 576, BFB), ("JK", 3456, BFB), ("AC", 24, F32),
    ("PL16", 2, U16), ("WKG", 160, F32), ("OKR", 96, BFB), ("FI", 32, F32),
    ("WW", 10, F32), ("EQ", 128, F32), ("OX16", 2, U16), ("KI", 64, I32), ("GC", 3, F32), ("BI", 2, I32),
    ("RX", 4, F32), ("RL16", 4, U16), ("XG", 128, F32), ("RA16", 4, U16),
    ("UI", 32, I32), ("BS", 8, F32), ("CI", 128, I32), ("C16", 64, U16), ("DX", 1024, BFB), ("RX2", 1024, BFB), ("VG", 1024, BFB),
    ("KEY", 64, F32), ("KMI", 4, I32), ("NN", 4, F32), ("BB16", 4, U16), ("FLG", 64, BFB), ("WO", 320, F32), ("YO", V, F32),
]:
    _buf(_n, _c, _d)
_CHK = ["B%d" % k for k in range(NCH)] + [c + "%d" % k for c in "HDR" for k in range(NBF)]
for _n in _CHK: _buf(_n, 16 * CW, BFB)
for _t in range(RO):
    _buf("XQ%d" % _t, SL, BFB)
    _buf("QX%d" % _t, SL, BFB)
    _buf("WR%d" % _t, SL, F32)
    _buf("QW%d" % _t, SL, F32)
PART = {}
for _k, _n in enumerate(("Z", "ZM", "Z2", "Z32", "ZM16", "ZY", "ZU", "ZV", "Z0")): PART[_n] = ("ZZ", 144 * _k, 144)
_buf("Z016", 144, BFB)
for _k, _n in enumerate(("LT", "GR2", "G016", "G32", "GN", "RS", "RS32", "RSN", "YR", "YRN", "GR", "I8", "I8N", "US", "PL", "GR3", "PLN")): PART[_n] = ("MX", 128 * _k, 128)
for _n, _b, _w, _l in (("HXA", "HX", 128, 0), ("HXB", "HX", 128, 1), ("A1", "AJ", 32, 1), ("A2", "AJ", 32, 2), ("AJ0", "AJ", 32, 0),
                       ("WG", "WKG", 32, 0), ("KG", "WKG", 32, 1), ("WK", "WKG", 32, 2), ("KK", "WKG", 32, 3), ("WDG", "WKG", 32, 4),
                       ("OG", "OKR", 32, 0), ("KL", "OKR", 32, 1), ("OR", "OKR", 32, 2), ("EQ1", "EQ", 64, 0), ("EQ2", "EQ", 64, 1),
                       ("W2", "WW", 2, 0), ("DU", "WW", 2, 1), ("DE", "WW", 2, 2), ("DE2", "WW", 2, 3), ("OX", "WW", 2, 4),
                       ("KI1", "KI", 32, 0), ("KD", "KI", 32, 1), ("LM", "LIM", 1, 0), ("LB0", "LIM", 1, 1),
                       ("GC1", "GC", 1, 0), ("GP", "GC", 1, 1), ("GS", "GC", 1, 2), ("BI1", "BI", 1, 0), ("BJ", "BI", 1, 1),
                       ("XG1", "XG", 64, 0), ("XD", "XG", 64, 1),
                       ("UI1", "UI", 4, 0), ("UA", "UI", 4, 1), ("UU", "UI", 4, 2), ("UV", "UI", 4, 3), ("MI", "UI", 4, 4), ("MJ", "UI", 4, 5), ("P2", "UI", 4, 6), ("P3", "UI", 4, 7),
                       ("BS1", "BS", 4, 0), ("TM", "BS", 4, 1), ("CI1", "CI", 64, 0), ("CA", "CI", 64, 1),
                       ("KM1", "KMI", 4, 0),
                       ("WO1", "WO", 64, 0), ("MK", "WO", 64, 1), ("FM", "WO", 64, 2), ("DW", "WO", 64, 3), ("DM", "WO", 64, 4),
                       ("YI0", "YI", 64, 0), ("YJ", "YI", 64, 1), ("Y2", "YI", 64, 2), ("Y3", "YI", 64, 3), ("Y4", "YI", 64, 4), ("Y5", "YI", 64, 5), ("Y6", "YI", 64, 6)):
    PART[_n] = (_b, _w * _l, _w)


def _pack(name, parts):
    d, a = SCRATCH[parts[0]][2], 0
    for p in parts:
        w = SCRATCH.pop(p)[1][1]
        PART[p] = (name, a, w)
        a += w
    _buf(name, a, d)


_pack("REQ", ["XQ%d" % t for t in range(RO)] + ["QX%d" % t for t in range(RO)])
_pack("REP", ["WR%d" % t for t in range(RO)] + ["QW%d" % t for t in range(RO)])
_pack("CHK", _CHK)
_pack("CF", ["JR", "ZR", "DG", "TR", "M64", "M16", "RI", "CO", "RB", "RC", "RE", "PC", "PC1"])
_pack("CB", ["BR", "ER", "CMI", "CMJ", "GK", "GG", "ID", "ON"])
PS = ["DA_", "DB_", "HA_", "HB_", "VA_", "VB_", "LA", "LB"]
for _n in PS:
    _buf(_n, 512, F32, "psum")
NDMA = 24
SEMAPHORES = ["sV", "sS", "sT", "sG", "loc"] + ["dm%d" % k for k in range(NDMA)] + ["rq%d" % t for t in range(RO)] + ["rp%d" % t for t in range(RO)]


def rank_program(g, core, T, topo):
    rank = T.rank_of(core)
    if rank is None:
        return
    n_ranks = len(T.cores)
    QS = {"V": g.vector, "S": g.scalar, "T": g.tensor, "G": g, "Y": g.sync}
    cnt = {q: 0 for q in QS}
    clk = {q: {} for q in QS}
    snap, hist, bank, extra = {}, {}, {}, {}
    ndma = [0]

    def R(n, a=0, b=None, s=1, ps=None, tag=None):
        if n in PART:
            n, o, w = PART[n]
            a, b = a + o, o + (w if b is None else b)
        elif b is None: b = SCRATCH[n][1][1]
        ap = T[n][:, a:b:s] if ps is None else T[n][ps, a:b:s]
        return ap, [(n, a, b, s, tag)]

    def IX(win, off):
        return win[0].indirect(off[0]), win[1] + off[1]

    def HBM(ap):
        return ap, []

    def overlap(x, y):
        if x[1] >= y[2] or y[1] >= x[2]: return False
        if x[4] is not None and y[4] is not None and x[4] != y[4]: return False
        return not (x[3] == y[3] > 1 and (x[1] - y[1]) % x[3])

    def learn(q, ev):
        c = clk[q]
        for k, v in list(snap.get(ev, {}).items()) + [ev]:
            if c.get(k, 0) < v: c[k] = v

    nodes, sent = [], {}

    def emit(q, fn, rd, wr, cost, dma=False, count=None, then=0.0, before=()):
        nodes.append([q, [(fn, rd, wr, dma, count)], rd, wr, cost, then, before])
        return len(nodes) - 1

    def schedule():
        n = len(nodes)
        succ, npred = [[] for _ in range(n)], [0] * n
        last, seen = {}, {}
        for i, (q, calls, rd, wr, cost, then, before) in enumerate(nodes):
            pred = {b: True for b in before}
            for regs, w in ((rd, False), (wr, True)):
                for r in regs:
                    if r[0] in PS:
                        for j, oq, ow in last.get(r[0], []):
                            if j != i and (w or ow or oq != q): pred[j] = pred.get(j, False) or oq != q
                    else:
                        for j, ow, reg in seen.get(r[0], []):
                            if j != i and (w or ow) and overlap(r, reg): pred[j] = True
            for regs, w in ((rd, False), (wr, True)):
                for r in regs:
                    if r[0] in PS:
                        h = last.setdefault(r[0], [])
                        if w: h[:] = [x for x in h if x[0] == i]
                        h.append((i, q, w))
                    else:
                        h = seen.setdefault(r[0], [])
                        if w and r[4] is None and r[3] == 1: h[:] = [x for x in h if x[0] == i or not (r[1] <= x[2][1] and x[2][2] <= r[2])]
                        h.append((i, w, r))
            npred[i] = len(pred)
            for j, wait in pred.items(): succ[j].append((i, wait))
        prec = [[] for _ in range(n)]
        for i in range(n):
            for k, (j, w) in enumerate(succ[i]):
                d = nodes[i][5] + WK if w else 0.0
                succ[i][k] = (j, d)
                prec[j].append((i, d))
        far = [0.0] * n
        for i in range(n - 1, -1, -1):
            far[i] = nodes[i][4] + max([far[j] + d for j, d in succ[i]] or [nodes[i][5]])

        def listed(edges, back, prio):
            left, at, end, order = [len(x) for x in back], [0.0] * n, [0.0] * n, []
            ready, free = {}, {}
            for i in range(n):
                if left[i] == 0: ready.setdefault(nodes[i][0], []).append(i)
            for _ in range(n):
                best = None
                for q, l in ready.items():
                    if not l: continue
                    t0 = max(free.get(q, 0.0), min([at[i] for i in l]))
                    if best is None or t0 < best[0]: best = (t0, q)
                t0, q = best
                l = ready[q]
                i = max([i for i in l if at[i] <= t0 + LOOK], key=lambda i: prio[i])
                l.remove(i)
                t1 = max(t0, at[i])
                order.append((t1, i))
                end[i] = t1 + nodes[i][4]
                if q != "N": free[q] = end[i]
                for j, d in edges[i]:
                    at[j] = max(at[j], end[i] + d)
                    left[j] -= 1
                    if left[j] == 0: ready.setdefault(nodes[j][0], []).append(j)
            return order, end

        if "order" not in MADE:
            prio, best, seed = far, None, 1
            for k in range(PASSES):
                order, end = listed(succ, prec, prio)
                if best is None or max(end) < best[0]: best = (max(end), order, prio)
                prio = listed(prec, succ, end)[1]
                if k % 4 == 3:
                    prio = []
                    for i in range(n):
                        seed = seed * 1103515245 + 12345 & 0x7fffffff
                        prio.append(best[2][i] + NOISE * ((seed >> 8) % 1000) / 1000.0)
            MADE["order"] = best[1]
        for _, i in MADE["order"]:
            q, calls = nodes[i][0], nodes[i][1]
            for fn, rd, wr, dma, count in calls:
                if q == "N": fn()
                else: issue(q, fn, rd, wr, dma, count)

    def issue(q, fn, rd, wr, dma=False, count=None):
        deps = {}

        def dep(ev):
            if clk[q].get(ev[0], 0) < ev[1] and deps.get(ev[0], 0) < ev[1]: deps[ev[0]] = ev[1]
        for regs, w in ((rd, False), (wr, True)):
            for r in regs:
                if r[0] in PS:
                    for oq, ev in bank.get(r[0], {}).items():
                        if oq != q: dep(ev)
                    continue
                for ev, oq, odma, ow, reg in hist.get(r[0], []):
                    if not (w or ow) or not overlap(r, reg): continue
                    dep(ev)
        evs = list(deps.items())
        for ev in evs:
            if any(o != ev and snap.get(o, {}).get(ev[0], 0) >= ev[1] for o in evs): continue
            QS[q].wait_ge(T.sem[ev[0] if ev[0] not in QS else "s" + ev[0]], ev[1])
        for ev in evs: learn(q, ev)
        ins = fn()
        if count is not None:
            return
        if dma:
            name = "dm%d" % ndma[0]
            ndma[0] += 1
            ins.then_inc(T.sem[name], 16)
            ev = (name, 16)
        else:
            cnt[q] += 1
            ins.then_inc(T.sem["s" + q], 1)
            ev = (q, cnt[q])
        snap[ev] = dict(clk[q])
        for regs, w in ((rd, False), (wr, True)):
            for r in regs:
                if r[0] in PS:
                    bank.setdefault(r[0], {})[q] = ev
                    continue
                h = hist.setdefault(r[0], [])
                if w and r[4] is None and r[3] == 1:
                    h[:] = [x for x in h if not (r[1] <= x[4][1] and x[4][2] <= r[2])]
                elif not w:
                    h[:] = [x for x in h if not (x[1] == q and not dma and not x[2] and not x[3] and x[4] == r)]
                h.append((ev, q, dma, w, r))

    def landed(name, sem, n):
        r = R(name)[1]
        emit("N", lambda: hist.setdefault(r[0][0], []).append(((sem, n), "net", True, True, r[0])), [], r, 0.1, then=2.0, before=(sent[sem],))

    def cols(x): return (x[1][-1][2] - x[1][-1][1] + x[1][-1][3] - 1) // x[1][-1][3] * (16 if len(x[1]) > 1 else 1)

    def narrow(*xs): return all(x[1][0][0] not in PS and SCRATCH[x[1][0][0]][2] in (BFB, U16) for x in xs)

    def vc(x, per): return 0.05 + cols(x) * GAT * CY if len(x[1]) > 1 else max(64.0, cols(x) * per) * CY

    def tt(o, x, y, op):
        emit("V", lambda: g.vector.tensor_tensor(o[0], x[0], y[0], op), x[1] + y[1], o[1], vc(x, 1 if x[1][0][0] in PS or y[1][0][0] in PS else 2))

    def ts(o, x, s1, op, s2=None, op1=None):
        rd, c = list(x[1]), []
        for s in (s1, s2):
            if isinstance(s, tuple):
                rd += s[1]
                c.append(s[0])
            else: c.append(s)
        w = vc(x, 0.5 if narrow(o, x) else 1)
        if op1 is None: emit("V", lambda: g.vector.tensor_scalar(o[0], x[0], c[0], None, op), rd, o[1], w)
        else: emit("V", lambda: g.vector.tensor_scalar(o[0], x[0], c[0], c[1], op, op1), rd, o[1], w)

    def cp(o, x): emit("V", lambda: g.vector.tensor_copy(o[0], x[0]), x[1], o[1], vc(x, 0.5 if narrow(o, x) else 1))
    def fill(o, v): emit("V", lambda: g.vector.memset(o[0], v), [], o[1], vc(o, 0.5 if narrow(o) else 1))
    def red(o, x, op): emit("V", lambda: g.vector.tensor_reduce(o[0], x[0], AxisListType.X, op), x[1], o[1], vc(x, 1))

    def scan(o, x, y, init, op0, op1):
        rd, i = x[1] + y[1], init
        if isinstance(init, tuple):
            rd, i = rd + init[1], init[0]
        emit("V", lambda: g.vector.tensor_tensor_scan(o[0], x[0], y[0], i, op0, op1), rd, o[1], vc(x, 0.5 if narrow(o, x, y) else 1))

    def scatter(win, off, x):
        emit("V", lambda: g.vector.tensor_copy(win[0].indirect(off[0]), x[0]), x[1] + off[1], win[1], 0.05 + cols(x) * SCA * CY)

    def act(o, x, f, bias=None, scale=1.0, acc=None):
        rd, kw, wr = list(x[1]), {"scale": scale}, list(o[1])
        for k, v in (("bias", bias), ("scale", scale)):
            if isinstance(v, tuple):
                rd += v[1]
                kw[k] = v[0]
            elif v is not None: kw[k] = v
        if acc is not None:
            wr += acc[1]
            kw["accum_out"] = acc[0]
        emit("S", lambda: g.scalar.activation(o[0], x[0], f, **kw), rd, wr, vc(x, 1) + 0.02)

    def sc(o, x, v): act(o, x, AF.Copy, scale=v)

    def mms(o, lrs, first, last):
        calls, rds, w = [], [], 0.0
        for k, (l, r) in enumerate(lrs):
            st, sp = first and k == 0, last and k == len(lrs) - 1
            calls.append((lambda l=l, r=r, st=st, sp=sp: g.tensor.matmul(o[0], l[0], r[0], st, sp), l[1] + r[1], o[1], False, None))
            rds += l[1] + r[1]
            w += max(64, cols(r)) * PEC * (4 if SCRATCH[l[1][0][0]][2] == F32 else 1)
        nodes.append(["T", calls, rds, o[1], w, 0.0, ()])

    def mm(o, l, r, start, stop): mms(o, [(l, r)], start, stop)

    def dma(q, o, x):
        w = sum((r[2] - r[1]) * (4 if SCRATCH[r[0]][2] in (F32, I32) else 2) * 128 for r in (o[1] or x[1])[:1]) / 2.0e5
        emit(q, lambda: QS[q].dma_start(o[0], x[0]), x[1], o[1], 0.1, dma=True, then=2.0 + w)

    def iota(o, pat, base, cm, small=True):
        w = 0.13 + 2 * cols(o) * CY
        if small: emit("G", lambda: g.iota(o[0], pat, base, cm, allow_small_or_imprecise_dtypes=True), [], o[1], w)
        else: emit("G", lambda: g.iota(o[0], pat, base, cm), [], o[1], w)

    def asel(o, x, pat, op, fillv, base, cm):
        emit("G", lambda: g.affine_select(o[0], x[0], pat, op, fillv, base, cm), x[1], o[1], 0.17 + 2 * cols(o) * CY)

    def wrapmm(out, n, src, first, last):
        b = PART[src][2] if src in PART else SCRATCH[src][1][1]
        mms(out, [(R(n, 15 - i, 143 - i), R(src, i, b, 16)) for i in range(16)], first, last)

    dma("Y", R("HS"), HBM(T.hy[:, :]))
    dma("S", R("VS"), HBM(T.vf[:, :]))
    dma("Y", R("RQ", 0, TY), HBM(T.rq[:, :]))
    dma("S", R("SG", 0, TY), HBM(T.sg[:, :]))
    dma("Y", R("WI"), HBM(T.wd[:, :]))
    dma("S", R("XS", 0, V), HBM(T.xs[:, :]))
    dma("Y", R("TH"), HBM(T.th[:, :]))

    iota(R("PI"), [[0, 1]], 0, 1, small=False)
    fill(R("ON"), 1.0)
    asel(R("GG"), R("ON"), [[-16, 8], [0, 16]], OP.is_ge, 0.0, 0, 1)
    asel(R("GG"), R("GG"), [[16, 8], [0, 16]], OP.is_ge, 0.0, 15, -1)
    fill(R("ST"), 0.0)
    ts(R("PA"), R("PI"), 15, OP.bitwise_and)
    cp(R("PC"), R("PA"))
    ts(R("PC1"), R("PC"), 1.0, OP.add)
    iota(R("CMI"), [[0, 8], [1, 16]], 0, 0)
    iota(R("BR"), [[1, NB]], 0, 0)
    iota(R("ER", 0, 96), [[16, 96]], 2560, 0)
    iota(R("ER", 96, NB), [[32, 64]], 4096, 0)
    iota(R("YI0"), [[1, 64]], 0, 64, small=False)
    iota(R("JR"), [[1, 512]], 0, 0)
    asel(R("ID"), R("ON"), [[-1, 128]], OP.is_equal, 0.0, 0, 1)
    asel(R("US"), R("GG"), [[1, 128]], OP.is_gt, 0.0, 0, -1)
    iota(R("M64"), [[1, 16], [0, 4]], 0, 0)
    iota(R("M16"), [[1, 16]], 0, 0)
    iota(R("XR0", LN, 576), [[1, 64]], 2560, 0)
    ts(R("RI"), R("CMI", 0, 16), R("PC"), OP.is_equal)

    def ri(p): return R("RI", p, p + 1)
    def co(k): return R("CO", k, k + 1)

    def role(k, pairs):
        for j, (p, v) in enumerate(pairs):
            if j: ts(co(k), ri(p), float(v), OP.mult, co(k), OP.add)
            else: ts(co(k), ri(p), float(v), OP.mult)

    ts(R("HXA"), R("HS"), 5, OP.arith_shift_right)
    cp(R("HB3", 0, 128), R("HXA"))
    ts(R("HXB"), R("HS"), 31, OP.bitwise_and)
    cp(R("HB3", 128, 256), R("HXB"))
    cp(R("HB3", 256, 384), R("VS"))
    for k, q in ((2, "S"), (0, "Y"), (1, "S")):
        dma(q, R("ST", 0, V, ps=slice(k, 128, 16), tag=k), R("HB3", 128 * k, 128 * k + 128))
    cp(R("GM"), R("GG", 0, 128, 16))
    ts(R("CMJ"), R("CMI"), 1.0, OP.add)
    tt(R("GK"), R("GG"), R("CMJ"), OP.mult)
    ts(R("GR2"), R("GK"), ri(2), OP.mult)
    for i in range(16): ts(R("WV", 128 * i, 128 * i + 128), R("GR2"), float(i + 1), OP.is_ge)
    ts(R("GR3"), R("GK"), ri(15), OP.mult)
    for i in range(16): ts(R("PWM", 128 * i, 128 * i + 128), R("GR3"), float(i + 2), OP.is_ge)
    sc(R("LT"), R("GG"), ri(15))
    fill(R("Z"), 0.0)
    cp(R("Z", 15, 143, 16), R("GM"))
    ts(R("ST", V, STW), R("ST", V, STW), ri(3), OP.add)
    fill(R("ZR"), 0.0)
    fill(R("FB", 0, LN), 0.0)
    ts(R("PIN", 128, NB), R("ZR", 0, 32), R("PC1"), OP.add)
    sc(R("Z0"), R("Z"), ri(0))
    sc(R("Z016"), R("Z0"), 16.0)
    role(1, [(0, 32), (1, 1), (3, 1024)])
    sc(R("ZY"), R("Z"), co(1))
    role(5, [(0, 16)])
    sc(R("G016"), R("GG"), co(5))
    fill(R("SG", TY, 1040), 0.0)
    fill(R("RQ", TY, 1040), TY)
    fill(R("XS", V, XSW), 0.0)
    fill(R("GTB"), 0.0)
    ts(R("GTB"), R("GTB"), ri(4), OP.add)
    ts(R("YJ"), R("YI0"), TY - 1, OP.bitwise_and)
    tt(R("Y2"), R("YJ"), R("YJ"), OP.mult)
    ts(R("Y3"), R("Y2"), 4, OP.arith_shift_right)
    ts(R("Y4"), R("YJ"), 5.0, OP.mult)
    tt(R("Y5"), R("Y3"), R("Y4"), OP.add)
    ts(R("Y6"), R("Y5"), 5, OP.arith_shift_right, 31, OP.bitwise_and)
    cp(R("YD", 0, 64), R("Y6"))
    ts(R("Y2"), R("Y5"), 31, OP.bitwise_and)
    cp(R("YD", 64, 128), R("Y2"))
    for k in range(2):
        dma("Y", R("GTB", 0, TY, ps=slice(k, 128, 16), tag=k), R("YD", 64 * k, 64 * k + 64))

    def consts2():
        sc(R("ZM"), R("Z"), -1.0)
        sc(R("Z2"), R("Z"), 2.0)
        sc(R("I8"), R("ID"), 8192.0)
        sc(R("I8N"), R("ID"), -8192.0)
        sc(R("G32"), R("GG"), 32.0)
        sc(R("GN"), R("GG"), -1.0)
        fill(R("RS"), 0.0)
        for k, v in ((0, 1.0), (1, 32.0), (2, -1.0)): ts(R("RS", k, 128, 16), R("GM"), v, OP.mult)
        sc(R("RS32"), R("RS"), 32.0)
        sc(R("RSN"), R("RS"), -1.0)
        for n in ("YR", "GR"): fill(R(n), 0.0)
        role(8, [(0, 1024), (1, 32)])
        role(9, [(0, 32768), (1, 1024)])
        for k, c in ((0, 8), (1, 9)): ts(R("YR", k, 128, 16), R("GM"), co(c), OP.mult)
        sc(R("YRN"), R("YR"), -1.0)
        ts(R("YR", 3, 128, 16), R("GM"), ri(3), OP.mult, 1024.0, OP.mult)
        role(12, [(0, 1024), (1, 32), (4, 31)])
        role(13, [(0, 32768), (1, 1024), (4, 992)])
        role(15, [(4, 1624)])
        for k, c in ((0, 12), (1, 13), (2, 15)): ts(R("GR", k, 128, 16), R("GM"), co(c), OP.mult)
        ts(co(14), R("PC"), 2.5, OP.is_gt, 1.0e9, OP.mult)
        for p, v in ((0, 100), (1, 3200), (2, -0.5)): ts(co(14), ri(p), float(v), OP.mult, co(14), OP.add)
        for k in range(4):
            ts(R("DG", 16 * k, 16 * k + 16), R("CMI", 0, 16), R("PC"), OP.is_equal)
            ts(R("RB", k, k + 1), R("PC"), 16.0 * k + 0.5, OP.add)
            ts(R("RC", k, k + 1), R("PC"), 16.0 * k, OP.add)
        for n in ("WF", "KF", "O0", "FF", "DA"): fill(R(n, LN, 576), 0.0)
        ts(R("LB0"), R("TH"), 8192.0, OP.add)
        cp(R("LM"), R("LB0"))

    def consts3():
        fill(R("WD", V, WDW), 0.0)
        fill(R("WD", MARK, MARK + 1), -1.0)
        fill(R("SVB"), 0.0)
        sc(R("Z32"), R("Z"), 32.0)
        sc(R("ZM16"), R("Z"), -16.0)
        ts(co(6), R("PC"), 10.0, OP.mult, 1.0, OP.add)
        sc(R("ZU"), R("Z"), co(6))
        role(7, [(2, -131072)])
        sc(R("ZV"), R("Z"), co(7))
        fill(R("RF"), 0.0)
        for k, v in ((0, 32.0), (1, 1024.0)): ts(R("RF", k, 128, 16), R("GM"), v, OP.mult)
        sc(R("GF"), R("GG"), 1.0)
        sc(R("SF"), R("ON"), ri(0))
        sc(R("PL"), R("US"), 2.0)
        tt(R("PL"), R("PL"), R("ID"), OP.subtract)
        sc(R("PLN"), R("PL"), -1.0)
        fill(R("NG", LN, 576), 1.0)
        fill(R("MN", LN, 576), -1.0)
        role(11, [(0, 32), (1, 1)])
        ts(R("YHM"), R("GM"), co(11), OP.mult)
        ts(R("RE", 0, 1), R("PC"), DUMP + 1.0 - 10000.0, OP.add)
        ts(R("RE", 1, 2), R("PC"), DUMP + 17.0 - 10000.0, OP.add)
        for k in range(2): ts(R("TR", 32 * k, 32 * k + 32), R("JR", 0, 32), R("RC", k, k + 1), OP.is_lt, 10000.0, OP.mult)

    def lanes(t):
        c = (ST0 * t) % V
        b0 = c // 16
        mms(R("LA", 0, 128), [(R("WV", 128 * i, 128 * i + 128), R("ST", i, V, 16)) for i in range(16)], True, True)
        if t: request(t - 1)
        ts(R("PIN", 0, 128 - b0), R("LA", b0, 128), -1.0, OP.mult, R("PC1"), OP.add)
        if b0: ts(R("PIN", 128 - b0, 128), R("LA", 0, b0), -1.0, OP.mult, R("PC1"), OP.add)
        mm(R("LB", 0, NB), R("LT"), R("PIN"), True, True)
        mms(R("LA", 0, 10), [(R("PWM", 128 * i, 128 * i + 128), R("PIN", i, NB, 16)) for i in range(16)], True, False)
        ts(R("EM"), R("LB", 0, NB), 0.0, OP.is_equal)
        tt(R("EMC"), R("EM"), R("ER"), OP.mult)
        scan(R("BPI"), R("LB", 0, NB), R("ZR"), 0.0, OP.add, OP.max)
        wrapmm(R("LA", 0, 10), "Z0", "EMC", False, True)
        tt(R("BPX"), R("BPI"), R("LB", 0, NB), OP.subtract)
        tt(R("OFF"), R("LA", 0, 10), R("BPX", 0, NB, 16), OP.add)
        cp(R("OF16"), R("OFF"))
        tt(R("PW"), R("BPX"), R("PIN"), OP.add)
        scatter(R("FB"), R("OF16"), R("BR"))
        scan(R("FR"), R("FB", 0, LN), R("FB", 0, LN), 0.0, OP.max, OP.max)
        wrapmm(R("LB", 0, 32), "Z0", "FR", True, True)
        wrapmm(R("LA", 0, 32), "Z016", "FR", True, False)
        cp(R("FL16"), R("LB", 0, 32))
        tt(R("E"), IX(R("PW"), R("FL16")), R("JR"), OP.is_le)
        if c:
            ts(R("A1"), R("LB", 0, 32), float(128 - b0), OP.is_ge, -2048.0, OP.mult)
            ts(R("A2"), R("LB", 0, 32), 128.0, OP.is_ge, float(2048 - c), OP.mult)
            tt(R("AJ0"), R("A1"), R("A2"), OP.add)
            mm(R("LA", 0, 32), R("ID"), R("AJ0"), False, False)
        wrapmm(R("LA", 0, 32), "Z", "E", False, True)
        ts(R("A16"), R("LA", 0, 32), float(c), OP.add)
        if t: service0(t - 1)
        cp(R("YG"), IX(R("ST"), R("A16")))
        wrapmm(R("LB", 0, 32), "ZY", "YG", True, True)
        mm(R("VA_"), R("G016"), R("FR"), True, False)
        if c:
            ts(R("AR", 0, 512), R("FR"), float(128 - b0), OP.is_ge, -2048.0, OP.mult)
            ts(R("AR", 512, 1024), R("FR"), 128.0, OP.is_ge, float(2048 - c), OP.mult)
            for k in range(2): mm(R("VA_"), R("ID"), R("AR", 512 * k, 512 * k + 512), False, False)
        mm(R("VA_"), R("GG"), R("E"), False, True)
        if t: service1(t - 1)
        act(R("XR0", 0, LN), R("VA_"), AF.Identity, bias=float(c))
        fill(R("FB", 0, LN), 0.0)

    def types(k):
        a, b = k * CW, k * CW + CW
        cp(R("KF", a, b), IX(R("RQ"), R("Y16", a // 16, b // 16)))
        cp(R("K16", a, b), R("KF", a, b))

    def typed(k):
        types(k)
        sgather(k)

    def words(k):
        a, b = k * CW, k * CW + CW
        cp(R("WF", a, b), IX(R("WD"), R("A16", a // 16, b // 16)))
        cp(R("W16", a, b), R("WF", a, b))

    def dbank(k): return R("DB_" if k % 2 else "DA_", 0, CW)
    def hbank(k): return R("HB_" if k % 2 else "HA_", 0, CW)
    def nbank(k, j): return R(NBK[k % len(NBK)], j * CW, j * CW + CW)

    def sgather(k):
        act(R("B%d" % k), IX(R("SG"), R("K16", k * CW, k * CW + CW)), AF.Copy)

    def hgather(k):
        act(R("H%d" % (k % NBF)), IX(R("ST"), R("W16", k * CW, k * CW + CW)), AF.Copy)

    def diff(k):
        tt(R("D%d" % (k % NBF)), IX(R("XS"), R("W16", k * CW, k * CW + CW)), R("B%d" % k), OP.subtract)

    def dsum1(k):
        if k in AS: act(R("R%d" % (k % NBF)), R("D%d" % (k % NBF)), AF.Abs)
        else: wrapmm(dbank(k), "ZM", "D%d" % (k % NBF), True, False)

    def dsum2(k):
        if k not in AS: ts(R("R%d" % (k % NBF)), R("D%d" % (k % NBF)), 0.0, OP.max)
        wrapmm(dbank(k), "Z" if k in AS else "Z2", "R%d" % (k % NBF), k in AS, False)

    def other(k):
        a, b = k * CW, k * CW + CW
        wrapmm(hbank(k), "ZY", "H%d" % (k % NBF), True, True)
        tt(R("O0", a, b), hbank(k), R("KF", a, b), OP.not_equal)
        mm(dbank(k), R("I8N"), R("DA", a, b), False, False)
        mm(dbank(k), R("I8"), R("O0", a, b), False, True)

    def verdict1(k):
        ts(R("FF", k * CW, k * CW + CW), dbank(k), R("LM"), OP.is_gt)

    def verdict2(k):
        a, b = k * CW, k * CW + CW
        hx = nbank(k, 1)
        for o, (m32, mn, m1) in ((R("VA_", a, b), ("G32", "GN", "GG")), (nbank(k, 0), ("RS32", "RSN", "RS")), (hx, ("RS32", "RSN", "RS"))):
            mm(o, R(mn), R("O0", a, b), True, False)
            mm(o, R(m1), R("DA", a, b), False, False)
            mm(o, R(m32), R("FF", a, b), False, o is not hx)
        mm(hx, R("GR"), R("GB", a, b), False, False)
        mm(hx, R("YRN"), R("YG", a, b), False, True)
        mm(nbank(k, 2), R("YR"), R("YG", a, b), True, True)

    def outcome(k):
        a, b = k * CW, k * CW + CW
        ts(R("PM", a, b), R("VA_", a, b), 0.0, OP.is_lt)
        scan(R("PP", a, b), R("PM", a, b), R("PM", a, b), R("PP", a - 1, a) if k else 0.0, OP.add, OP.max)
        ts(R("MU", a, b), nbank(k, 0), co(14), OP.is_gt)
        tt(R("T2", a, b), nbank(k, 1), R("MU", a, b), OP.mult)
        tt(R("QQ", a, b), nbank(k, 2), R("T2", a, b), OP.add)
        ts(R("DD", a, b), R("QQ", a, b), 10, OP.arith_shift_right, 31, OP.bitwise_and)

    def proposals_part(j):
        a, b = PARTS[j], PARTS[j + 1]
        for k in range(2):
            act(R("JK", 576 * k + a, 576 * k + b), R("PP", a, b), AF.Sign, bias=R("RB", k, k + 1), scale=-1.0, acc=R("AC", 8 * j + k, 8 * j + k + 1))

    def repairs_part(j):
        a, b = PARTS[j], PARTS[j + 1]
        act(R("NG", a, b), R("VA_", a, b), AF.Sign, bias=-0.5, acc=R("AC", 8 * j + 6, 8 * j + 7))
        act(R("MN", a, b), R("VA_", a, b), AF.Sign, bias=-100.0)
        if j: b += SL
        scan(R("RP", a, b), R("NG", a, b), R("MN", a, b), R("RP", a - 1, a) if j else 0.0, OP.add, OP.subtract)
        for k in range(4):
            act(R("JK", 576 * k + 1152 + a, 576 * k + 1152 + b), R("RP", a, b), AF.Sign, bias=R("RB", k, k + 1), scale=-0.5, acc=R("AC", 8 * j + 2 + k, 8 * j + 3 + k))

    def lanes_part(j):
        a, b = PARTS[j], PARTS[j + 1]
        scatter(R("ST"), R("A16", a // 16, b // 16), R("DD", a, b))

    def retypes():
        tt(R("AC", 16, 18), R("AC", 0, 2), R("AC", 8, 10), OP.add)
        ts(R("PL16"), R("AC", 16, 18), 0.5, OP.mult, 256.0, OP.add)
        cp(R("OG"), IX(R("O0"), R("PL16")))
        cp(R("KG"), IX(R("KF"), R("PL16")))
        cp(R("WG"), IX(R("WF"), R("PL16")))
        cp(R("KL"), IX(R("DA"), R("PL16")))
        mm(R("LA", 0, 32), R("PL"), R("OG"), True, False)
        mm(R("LA", 0, 32), R("PLN"), R("KL"), False, True)
        ts(R("WG"), R("WG"), float(-DUMP), OP.add)
        ts(R("FI"), R("LA", 0, 32), 0.0, OP.is_lt)
        tt(R("WK"), R("WG"), R("FI"), OP.mult)
        tt(R("KK"), R("KG"), R("FI"), OP.mult)
        mm(R("LA", 0, 32), R("GF"), R("WK"), True, True)
        mm(R("LB", 0, 32), R("RF"), R("KK"), True, True)
        tt(R("WDG"), R("LA", 0, 32), R("DG", 0, 32), OP.mult)
        for k in range(2): red(R("W2", k, k + 1), R("WDG", 16 * k, 16 * k + 16), OP.add)
        for k in range(2): ts(R("EQ1", 32 * k, 32 * k + 32), R("LA", 0, 32), R("W2", k, k + 1), OP.is_equal)
        tt(R("EQ2"), R("EQ1"), R("TR"), OP.mult)
        cp(R("KI1"), R("LB", 0, 32))
        for k in range(2): red(R("DU", k, k + 1), R("EQ2", 32 * k, 32 * k + 32), OP.max)
        ts(R("KD"), R("KI1"), 10, OP.arith_shift_right, 31, OP.bitwise_and)
        ts(R("DE"), R("W2"), float(DUMP), OP.add)
        for k in range(2): ts(R("OX16", k, k + 1), R("DU", k, k + 1), R("RE", k, k + 1), OP.add, R("DE", k, k + 1), OP.max)
        scatter(R("ST"), R("OX16"), R("KD"))

    def count_good():
        tt(R("AC", 22, 23), R("AC", 6, 7), R("AC", 14, 15), OP.add)
        ts(R("GC1"), R("AC", 22, 23), -0.5, OP.mult, 256.0, OP.add)
        tt(R("GS"), R("GC1"), R("GP"), OP.subtract)
        mm(R(GBK, 0, 1), R("SF"), R("GS"), True, True)
        cp(R("BI1"), R(GBK, 0, 1))
        ts(R("BJ"), R("BI1"), 255, OP.bitwise_and)
        tt(R("LM"), R("LB0"), R("BJ"), OP.add)

    def send(buf, land, dst, sem):
        eng = topo.engines(core, dst)[:8]
        mask = sum(1 << e for e in eng)
        rid, pid, _ = topo.addr(dst)
        x, y = R(buf), R(land)
        sent[sem] = emit("G", lambda: g.remote_dma(y[0], x[0], T.sem[sem], T.sem.loc, pid, rid, mask), x[1], [], 1.0, count=len(eng))
        extra["loc"] = extra.get("loc", 0) + len(eng)

    def helper(t): return T.cores[(rank + 1 + t % (n_ranks - 1)) % n_ranks]
    def asker(t): return T.cores[(rank - 1 - t % (n_ranks - 1)) % n_ranks]

    def request(t):
        tt(R("AC", 18, 22), R("AC", 2, 6), R("AC", 10, 14), OP.add)
        ts(R("RL16"), R("AC", 18, 22), 0.5, OP.mult, 288.0, OP.add)
        cp(R("XG1"), IX(R("XR0"), R("RL16")))
        tt(R("XD"), R("XG1"), R("DG"), OP.mult)
        for k in range(4): red(R("RX", k, k + 1), R("XD", 16 * k, 16 * k + 16), OP.add)
        cp(R("RA16"), R("RX"))
        cp(R("XQ%d" % t), IX(R("XS"), R("RA16")))
        send("XQ%d" % t, "QX%d" % t, helper(t), "rq%d" % t)

    def service0(t):
        X = "QX%d" % t
        landed(X, "rq%d" % t, len(topo.engines(asker(t), core)[:8]))
        wrapmm(R(UB, 0, 4), "ZU", X, True, True)

    def service1(t):
        cp(R("UI1"), R(UB, 0, 4))
        ts(R("UA"), R("UI1"), V - 1, OP.bitwise_and)
        tt(R("UU"), R("UA"), R("UA"), OP.mult)
        ts(R("TM"), R("UA"), 2.0, OP.mult, 1.0, OP.add)
        ts(R("UV"), R("UU"), 5, OP.arith_shift_right)
        tt(R("BS1"), R("UV"), R("UA"), OP.add)
        for k in range(4):
            ts(R("CI1", k, 64, 4), R("M16"), R("TM", k, k + 1), OP.mult, R("BS1", k, k + 1), OP.add)
        ts(R("CA"), R("CI1"), V - 1, OP.bitwise_and)
        cp(R("C16"), R("CA"))
        act(R("VG"), IX(R("SVB"), R("C16")), AF.Copy)

    def service2(t, a=0, b=16):
        X = "QX%d" % t
        for m in range(a, b):
            tt(R("DX", 64 * m, 64 * m + 64), IX(R("XS"), R("C16", 4 * m, 4 * m + 4)), R(X), OP.subtract)
        if b == 16:
            ts(R("RX2"), R("DX"), 0.0, OP.max)
            wrapmm(R(KB, 0, 64), "ZV", "VG", True, False)
            wrapmm(R(KB, 0, 64), "ZM16", "DX", False, False)
            wrapmm(R(KB, 0, 64), "Z32", "RX2", False, True)

    def service3(t):
        tt(R("KEY"), R(KB, 0, 64), R("M64"), OP.add)
        for k in range(4): red(R("KM1", k, k + 1), R("KEY", k, 64, 4), OP.min)
        ts(R("NN"), R("KM1"), 0.0, OP.is_ge, 4096.0, OP.mult)
        ts(R("MJ"), R("KM1"), 15, OP.bitwise_and)
        for k in range(4): ts(R("P2", k, k + 1), R("MJ", k, k + 1), R("TM", k, k + 1), OP.mult, R("BS1", k, k + 1), OP.add)
        ts(R("P3"), R("P2"), V - 1, OP.bitwise_and)
        for k in range(4): ts(R("BB16", k, k + 1), R("P3", k, k + 1), R("NN", k, k + 1), OP.add, float(MARK), OP.min)
        cp(R("WR%d" % t), IX(R("WD"), R("BB16")))
        send("WR%d" % t, "QW%d" % t, asker(t), "rp%d" % t)

    def merge(t):
        W = "QW%d" % t
        cp(R("WO1"), IX(R("WD"), R("RA16")))
        cp(R("FLG"), IX(R("FF"), R("RL16")))
        landed(W, "rp%d" % t, len(topo.engines(helper(t), core)[:8]))
        ts(R("MK"), R(W), 0.0, OP.is_ge)
        tt(R("DW"), R(W), R("WO1"), OP.subtract)
        tt(R("FM"), R("MK"), R("FLG"), OP.mult)
        tt(R("DM"), R("DW"), R("FM"), OP.mult)
        win, off, x, y = R("WD"), R("RA16"), R("WO1"), R("DM")
        emit("V", lambda: g.vector.tensor_tensor(win[0].indirect(off[0]), x[0], y[0], OP.add), x[1] + y[1] + off[1], win[1], 0.05 + SL * SCA * CY)

    for t in range(RO):
        if t == 0: consts2()
        lanes(t)
        if t: service2(t - 1, 0, 6)
        cp(R("Y16"), R("LB", 0, 32))
        for k in range(TF[0]): typed(k)
        if t: service2(t - 1, 6, 16)
        for k in range(TF[0], TF[1]): typed(k)
        if t == 0:
            consts3()
            cp(R("WD", 0, V), R("WI"))
        else:
            service3(t - 1)
        for k in range(TF[1], NCH): types(k)
        ts(R("DA", 0, LN), R("K16"), float(TY), OP.is_equal)
        dma("Y", R("SVB", 0, V, ps=slice(2, 128, 16)), R("ST", 0, V, ps=slice(2, 128, 16)))
        if t: count_good()
        ts(R("GP"), R("BPI", 127, 128), -1.0, OP.mult, float(LN), OP.add)
        ts(R("GP"), R("GP"), 0.0, OP.max)
        act(R("GB"), IX(R("GTB"), R("Y16")), AF.Copy)
        if t: merge(t - 1)
        for k in range(TF[1], SB): sgather(k)
        for k in range(NCH + 1):
            if k < NCH:
                words(k)
                hgather(k)
                if k + SB < NCH: sgather(k + SB)
                diff(k)
            if k: other(k - 1)
            if k < NCH: dsum1(k)
            if k > 1: outcome(k - 2)
            if k: verdict1(k - 1)
            if k < NCH: dsum2(k)
            if k: verdict2(k - 1)
            if k > 1 and k - 1 == PARTS[1] // CW:
                proposals_part(0)
                repairs_part(0)
        outcome(NCH - 1)
        lanes_part(0)
        proposals_part(1)
        repairs_part(1)
        if t == RO - 1: request(t)
        lanes_part(1)
        retypes()
    service0(RO - 1)
    service1(RO - 1)
    service2(RO - 1)
    service3(RO - 1)
    for k in range(4):
        mm(R(PS[k], 0, 512, ps=slice(0, 8)), R("YHM"), R("ST", 512 * k, 512 * k + 512), True, True)
        act(R("YO", 512 * k, 512 * k + 512, ps=slice(0, 8)), R(PS[k], 0, 512, ps=slice(0, 8)), AF.Copy)
    dma("Y", HBM(T.yh[:, :]), R("YO", 0, V, ps=slice(0, 8)))
    dma("G", HBM(T.yv[:, :]), R("ST", 0, V, ps=slice(2, 128, 16)))
    merge(RO - 1)
    dma("Y", HBM(T.ym[:, :]), R("WD", 0, V))
    schedule()
    for q in ("V", "S", "T", "G"):
        g.wait_ge(T.sem["s" + q], cnt[q])
    for k in range(ndma[0]): g.wait_ge(T.sem["dm%d" % k], 16)
    g.wait_ge(T.sem.loc, extra["loc"])
